import numpy as np
import ml_dtypes


def mxq(x, axis, fmt="e4m3"):
    dtype, down = {"e4m3": (ml_dtypes.float8_e4m3fn, 7), "e5m2": (ml_dtypes.float8_e5m2, 14)}[fmt]
    v = np.moveaxis(np.asarray(x, np.float32).astype(ml_dtypes.bfloat16).astype(np.float64), axis, -1)
    blocks = v.reshape(v.shape[:-1] + (-1, 32))
    amax = np.abs(blocks).max(-1, keepdims=True)
    byte = np.maximum(np.where(amax > 0, np.frexp(amax)[1] - 1 + 127, 0) - down, 1)
    scale = np.exp2(byte - 127.0)
    codes = (blocks / scale).astype(np.float32).astype(dtype).astype(np.float64)
    return np.moveaxis((codes * scale).reshape(v.shape), -1, axis)


WIDE = False


def mx_kscale(k):
    if not WIDE:
        return np.ones(k)
    levels = np.array([30, -30])
    if k % 512:
        return np.exp2(np.random.permutation(np.resize(levels, k // 32))).repeat(32)
    a = np.empty((k // 512, 16))
    for p in range(k // 512):
        a[p, :8] = np.random.permutation(np.resize(levels, 8))
        for g in range(8):
            far = levels[np.abs(levels - a[p, g]) >= 10]
            a[p, g + 8] = far[np.random.randint(len(far))]
    return np.exp2(a.ravel()).repeat(32)


def f64(x):
    return np.asarray(x).astype(np.float64)


E2M1 = np.array([0.0, 0.5, 1.0, 1.5, 2.0, 3.0, 4.0, 6.0, -0.0, -0.5, -1.0, -1.5, -2.0, -3.0, -4.0, -6.0])


def pack_weight(w, fmt):
    k, n = w.shape
    w = f64(np.asarray(w, np.float32).astype(ml_dtypes.bfloat16)).reshape(k // 32, 32, n)
    amax = np.abs(w).max(1)
    if fmt == "e4m3":
        byte = np.frexp(amax)[1] - 1 + 127 - 7
    else:
        mant, ex = np.frexp(amax / 6.0)
        byte = np.where(mant > 0.5, ex, ex - 1) + 127
    byte = np.clip(np.where(amax > 0, byte, 1), 1, 254)
    scaled = (w * np.exp2(127.0 - byte)[:, None, :]).reshape(k, n).astype(np.float32)
    by_word = np.ascontiguousarray(scaled.reshape(k // 512, 128, 4, n).transpose(0, 1, 3, 2))
    if fmt == "e4m3":
        words = by_word.astype(ml_dtypes.float8_e4m3fn).view(np.uint8)
    else:
        c = by_word.astype(ml_dtypes.float4_e2m1fn).view(np.uint8) & 0xF
        words = (c[..., 0::2] | (c[..., 1::2] << 4)).reshape(k // 512, 128, 2 * n)
    return np.ascontiguousarray(words), np.ascontiguousarray(byte.astype(np.uint8).reshape(k // 512, 16, n))


def unpack_weight(words, scales, fmt):
    g, _, n = scales.shape
    words = np.ascontiguousarray(words).reshape(g, 128, n, -1)
    if fmt == "e4m3":
        vals = words.view(ml_dtypes.float8_e4m3fn).astype(np.float64)
    else:
        nib = np.empty((g, 128, n, 4), np.uint8)
        nib[..., 0::2] = words & 0xF
        nib[..., 1::2] = words >> 4
        vals = E2M1[nib]
    vals = vals * np.repeat(np.exp2(scales.astype(np.float64) - 127.0), 8, axis=1)[..., None]
    return vals.transpose(0, 1, 3, 2).reshape(g * 512, n)


O, K, M, T = 1024, 1536, 512, 1536


def setup_inputs():
    n = np.random.standard_normal
    s = mx_kscale(K)[:, None]
    dy = np.exp(0.5 * n((1, T))) * n((K, T))
    w = n((K, M)) / np.sqrt(K) / s
    p_w8 = pack_weight(w[:O], "e4m3")
    p_w4 = pack_weight(w[O:], "e2m1")
    return {
        "dy": (dy * s).astype(np.float32),
        "w8_words": p_w8[0],
        "w8_scales": p_w8[1],
        "w4_words": p_w4[0],
        "w4_scales": p_w4[1],
        "g": (n((1536, 512))).astype(np.float32),
    }


def reference(dy, w8_words, w8_scales, w4_words, w4_scales, g):
    dy_ = mxq(f64(dy), 0, "e5m2")
    w8_ = unpack_weight(w8_words, w8_scales, "e4m3")
    w4_ = unpack_weight(w4_words, w4_scales, "e2m1")
    y = dy_[:O].T @ w8_ + dy_[O:].T @ w4_
    return f64(g) * y

@@ -1,0 +1,134 @@
+from contextlib import ExitStack
+
+import concourse.mybir as mybir
+
+F32 = mybir.dt.float32
+BF16 = mybir.dt.bfloat16
+U32 = mybir.dt.uint32
+I32 = mybir.dt.int32
+U8 = mybir.dt.uint8
+E4M3X4 = mybir.dt.float8_e4m3fn_x4
+E5M2X4 = mybir.dt.float8_e5m2_x4
+E2M1X4 = mybir.dt.float4_e2m1fn_x4
+MULT = mybir.AluOpType.mult
+
+P = 128
+K, T, D = 1536, 1536, 512
+PASSES = 3
+TILES = T // P
+QUADS = TILES // 4
+
+FLOPS = 2 * K * T * D
+BYTES = 4 * K * T + 2 * 4 * T * D + 1024 * D + 512 * D // 2 + 48 * D
+
+STORES = ((4, 6), (6, 8), (8, 10), (10, 11), (11, 12))
+
+
+def tile_mix_dyq_tm_mul_kernel(tc, dy, w8_words, w8_scales, w4_words, w4_scales, g, out):
+    nc = tc.nc
+    with ExitStack() as ctx:
+        keep = ctx.enter_context(tc.tile_pool(name="keep", bufs=1))
+        psum = ctx.enter_context(tc.psum_pool(name="psum", bufs=1))
+        ctx.enter_context(tc.manual_schedule())
+
+        planes = keep.tile([P, PASSES, D], U8, name="planes", align_bytes=64)
+        w8 = keep.tile([P, 2, D], U32, name="w8", align_bytes=64)
+        w4 = keep.tile([P, 2 * D], U8, name="w4", align_bytes=64)
+        raw = [keep.tile([P, 4, T], F32, name="raw%d" % a, align_bytes=64) for a in range(PASSES)]
+        g_sb = keep.tile([P, TILES, D], F32, name="g_sb", align_bytes=64)
+        o_sb = keep.tile([P, TILES, D], F32, name="o_sb", align_bytes=64)
+        grouped = {}
+        codes = {}
+        scales = {}
+        for a in range(PASSES):
+            for q in range(QUADS):
+                grouped[a, q] = keep.tile([P, 4 * D], BF16, name="grouped%d_%d" % (a, q), align_bytes=64)
+                codes[a, q] = keep.tile([P, D], U32, name="codes%d_%d" % (a, q), align_bytes=64)
+                scales[a, q] = keep.tile([P, D], U8, name="scales%d_%d" % (a, q), align_bytes=64)
+
+        def load_dy(a):
+            nc.sync.dma_start(out=raw[a][:], in_=dy[512 * a : 512 * (a + 1), :].rearrange("(p j) t -> p j t", j=4))
+
+        nc.vector.memset(planes[:].bitcast(I32), 0)
+        load_dy(0)
+        for b in range(4):
+            nc.sync.dma_start(
+                out=planes[32 * b : 32 * b + 4, 0:2, :].bitcast(I32),
+                in_=w8_scales[:, 4 * b : 4 * b + 4, :].rearrange("a r n -> r a n").bitcast(I32),
+            )
+        nc.sync.dma_start(out=w8[:].bitcast(I32), in_=w8_words.rearrange("a p n t -> p a (n t)").bitcast(I32))
+        load_dy(1)
+        load_dy(2)
+        for b in range(4):
+            nc.sync.dma_start(
+                out=planes[32 * b : 32 * b + 4, 2, :].bitcast(I32),
+                in_=w4_scales[0, 4 * b : 4 * b + 4, :].bitcast(I32),
+            )
+        nc.sync.dma_start(out=w4[:].bitcast(I32), in_=w4_words[0].bitcast(I32))
+        g_view = g.rearrange("(p r) d -> p r d", r=TILES)
+        out_view = out.rearrange("(p r) d -> p r d", r=TILES)
+        for q in range(QUADS):
+            rows = slice(4 * q, 4 * q + 4)
+            nc.sync.dma_start(out=g_sb[:, rows, :], in_=g_view[:, rows, :])
+
+
+        def group(copy, a, q, m0, m1):
+            src = raw[a][:].rearrange("p j (m q i) -> p q m j i", q=QUADS, i=4)[:, q]
+            dst = grouped[a, q][:].rearrange("p (i m j) -> p m j i", i=4, j=4)
+            copy(out=dst[:, m0:m1], in_=src[:, m0:m1])
+
+        def quantise(a, q):
+            nc.vector.quantize_mx(out=codes[a, q][:].bitcast(E5M2X4), scales=scales[a, q][:], in_=grouped[a, q][:])
+
+        acc = {}
+
+        def multiply(a, r):
+            if a == 0:
+                acc[r] = psum.tile([P, D], F32, name="acc%d" % (r % 8))
+            cols = slice(P * (r % 4), P * (r % 4 + 1))
+            nc.tensor.matmul_mx(
+                out=acc[r][:],
+                lhsT=codes[a, r // 4][:, cols].bitcast(E5M2X4),
+                lhsT_scale=scales[a, r // 4][:, cols],
+                rhs=w8[:, a, :].bitcast(E4M3X4) if a < 2 else w4[:].bitcast(E2M1X4),
+                rhs_scale=planes[:, a, :],
+                start=(a == 0),
+                stop=(a == PASSES - 1),
+            )
+
+        def finish(r):
+            nc.vector.tensor_tensor(out=o_sb[:, r, :], in0=acc[r][:], in1=g_sb[:, r, :], op=MULT)
+
+        def store(lo, hi):
+            nc.sync.dma_start(out=out_view[:, lo:hi, :], in_=o_sb[:, lo:hi, :])
+
+        for a in range(PASSES):
+            group(nc.scalar.copy, a, 1, 0, P)
+            group(nc.scalar.copy, a, 2, 0, P)
+            group(nc.vector.tensor_copy, a, 0, 0, P)
+            quantise(a, 0)
+            if a < PASSES - 1:
+                quantise(a, 1)
+                quantise(a, 2)
+                for r in range(8):
+                    multiply(a, r)
+
+        for r in range(4):
+            multiply(2, r)
+        for r in range(4):
+            finish(r)
+            if r == 0:
+                quantise(2, 1)
+                for s in range(4, 8):
+                    multiply(2, s)
+            multiply(0, r + 8)
+            multiply(1, r + 8)
+            if r % 2:
+                store(r - 1, r + 1)
+        quantise(2, 2)
+        for r in range(8, TILES):
+            multiply(2, r)
+        for lo, hi in STORES:
+            for r in range(lo, hi):
+                finish(r)
+            store(lo, hi)

@@ -21,7 +21,8 @@ QUADS = TILES // 4
 FLOPS = 2 * K * T * D
 BYTES = 4 * K * T + 2 * 4 * T * D + 1024 * D + 512 * D // 2 + 48 * D
 
-STORES = ((4, 6), (6, 8), (8, 10), (10, 11), (11, 12))
+SPLIT = 32
+STORES = ((0, 4), (4, 7), (7, 10), (10, 12))
 
 
 def tile_mix_dyq_tm_mul_kernel(tc, dy, w8_words, w8_scales, w4_words, w4_scales, g, out):
@@ -31,7 +32,8 @@ def tile_mix_dyq_tm_mul_kernel(tc, dy, w8_words, w8_scales, w4_words, w4_scales,
         psum = ctx.enter_context(tc.psum_pool(name="psum", bufs=1))
         ctx.enter_context(tc.manual_schedule())
 
-        planes = keep.tile([P, PASSES, D], U8, name="planes", align_bytes=64)
+        planes8 = keep.tile([P, 2, D], U8, name="planes8", align_bytes=64)
+        plane4 = keep.tile([P, D], U8, name="plane4", align_bytes=64)
         w8 = keep.tile([P, 2, D], U32, name="w8", align_bytes=64)
         w4 = keep.tile([P, 2 * D], U8, name="w4", align_bytes=64)
         raw = [keep.tile([P, 4, T], F32, name="raw%d" % a, align_bytes=64) for a in range(PASSES)]
@@ -49,28 +51,25 @@ def tile_mix_dyq_tm_mul_kernel(tc, dy, w8_words, w8_scales, w4_words, w4_scales,
         def load_dy(a):
             nc.sync.dma_start(out=raw[a][:], in_=dy[512 * a : 512 * (a + 1), :].rearrange("(p j) t -> p j t", j=4))
 
-        nc.vector.memset(planes[:].bitcast(I32), 0)
+        nc.vector.memset(planes8[:].bitcast(I32), 0)
+        nc.vector.memset(plane4[:].bitcast(I32), 0)
         load_dy(0)
-        for b in range(4):
+        for r in range(4):
             nc.sync.dma_start(
-                out=planes[32 * b : 32 * b + 4, 0:2, :].bitcast(I32),
-                in_=w8_scales[:, 4 * b : 4 * b + 4, :].rearrange("a r n -> r a n").bitcast(I32),
+                out=planes8[r:P:32, :, :].bitcast(I32),
+                in_=w8_scales[:, r:16:4, :].rearrange("a q n -> q a n").bitcast(I32),
             )
         nc.sync.dma_start(out=w8[:].bitcast(I32), in_=w8_words.rearrange("a p n t -> p a (n t)").bitcast(I32))
         load_dy(1)
         load_dy(2)
-        for b in range(4):
-            nc.sync.dma_start(
-                out=planes[32 * b : 32 * b + 4, 2, :].bitcast(I32),
-                in_=w4_scales[0, 4 * b : 4 * b + 4, :].bitcast(I32),
-            )
+        for r in range(4):
+            nc.sync.dma_start(out=plane4[r:P:32, :].bitcast(I32), in_=w4_scales[0, r:16:4, :].bitcast(I32))
         nc.sync.dma_start(out=w4[:].bitcast(I32), in_=w4_words[0].bitcast(I32))
         g_view = g.rearrange("(p r) d -> p r d", r=TILES)
         out_view = out.rearrange("(p r) d -> p r d", r=TILES)
         for q in range(QUADS):
             rows = slice(4 * q, 4 * q + 4)
             nc.sync.dma_start(out=g_sb[:, rows, :], in_=g_view[:, rows, :])
-
 
         def group(copy, a, q, m0, m1):
             src = raw[a][:].rearrange("p j (m q i) -> p q m j i", q=QUADS, i=4)[:, q]
@@ -91,44 +90,42 @@ def tile_mix_dyq_tm_mul_kernel(tc, dy, w8_words, w8_scales, w4_words, w4_scales,
                 lhsT=codes[a, r // 4][:, cols].bitcast(E5M2X4),
                 lhsT_scale=scales[a, r // 4][:, cols],
                 rhs=w8[:, a, :].bitcast(E4M3X4) if a < 2 else w4[:].bitcast(E2M1X4),
-                rhs_scale=planes[:, a, :],
+                rhs_scale=planes8[:, a, :] if a < 2 else plane4[:],
                 start=(a == 0),
                 stop=(a == PASSES - 1),
             )
 
+        last_of = {hi - 1: lo for lo, hi in STORES}
+
         def finish(r):
             nc.vector.tensor_tensor(out=o_sb[:, r, :], in0=acc[r][:], in1=g_sb[:, r, :], op=MULT)
+            if r in last_of:
+                rows = slice(last_of[r], r + 1)
+                nc.sync.dma_start(out=out_view[:, rows, :], in_=o_sb[:, rows, :])
 
-        def store(lo, hi):
-            nc.sync.dma_start(out=out_view[:, lo:hi, :], in_=o_sb[:, lo:hi, :])
-
-        for a in range(PASSES):
+        for a in range(PASSES - 1):
             group(nc.scalar.copy, a, 1, 0, P)
             group(nc.scalar.copy, a, 2, 0, P)
             group(nc.vector.tensor_copy, a, 0, 0, P)
-            quantise(a, 0)
-            if a < PASSES - 1:
-                quantise(a, 1)
-                quantise(a, 2)
-                for r in range(8):
-                    multiply(a, r)
+            for q in range(QUADS):
+                quantise(a, q)
+            for r in range(8):
+                multiply(a, r)
 
-        for r in range(4):
+        group(nc.scalar.copy, 2, 1, SPLIT, P)
+        group(nc.scalar.copy, 2, 2, 0, P)
+        group(nc.vector.tensor_copy, 2, 0, 0, P)
+        group(nc.vector.tensor_copy, 2, 1, 0, SPLIT)
+        quantise(2, 0)
+        quantise(2, 1)
+        for r in range(8):
             multiply(2, r)
         for r in range(4):
             finish(r)
-            if r == 0:
-                quantise(2, 1)
-                for s in range(4, 8):
-                    multiply(2, s)
             multiply(0, r + 8)
             multiply(1, r + 8)
-            if r % 2:
-                store(r - 1, r + 1)
         quantise(2, 2)
         for r in range(8, TILES):
             multiply(2, r)
-        for lo, hi in STORES:
-            for r in range(lo, hi):
-                finish(r)
-            store(lo, hi)
+        for r in range(4, TILES):
+            finish(r)

@@ -104,10 +104,10 @@ def tile_mix_dyq_tm_mul_kernel(tc, dy, w8_words, w8_scales, w4_words, w4_scales,
                 nc.sync.dma_start(out=out_view[:, rows, :], in_=o_sb[:, rows, :])
 
         for a in range(PASSES - 1):
-            group(nc.scalar.copy, a, 1, 0, P)
             group(nc.scalar.copy, a, 2, 0, P)
+            group(nc.scalar.copy, a, 1, 0, P)
             group(nc.vector.tensor_copy, a, 0, 0, P)
-            for q in range(QUADS):
+            for q in (0, 2, 1):
                 quantise(a, q)
             for r in range(8):
                 multiply(a, r)
@@ -122,10 +122,9 @@ def tile_mix_dyq_tm_mul_kernel(tc, dy, w8_words, w8_scales, w4_words, w4_scales,
             multiply(2, r)
         for r in range(4):
             finish(r)
-            multiply(0, r + 8)
-            multiply(1, r + 8)
         quantise(2, 2)
         for r in range(8, TILES):
-            multiply(2, r)
+            for a in range(PASSES):
+                multiply(a, r)
         for r in range(4, TILES):
             finish(r)

@@ -22,7 +22,7 @@ FLOPS = 2 * K * T * D
 BYTES = 4 * K * T + 2 * 4 * T * D + 1024 * D + 512 * D // 2 + 48 * D
 
 SPLIT = 32
-STORES = ((0, 4), (4, 7), (7, 10), (10, 12))
+STORES = ((0, 3), (3, 6), (6, 8), (8, 10), (10, 12))
 
 
 def tile_mix_dyq_tm_mul_kernel(tc, dy, w8_words, w8_scales, w4_words, w4_scales, g, out):
@@ -120,11 +120,12 @@ def tile_mix_dyq_tm_mul_kernel(tc, dy, w8_words, w8_scales, w4_words, w4_scales,
         quantise(2, 1)
         for r in range(8):
             multiply(2, r)
-        for r in range(4):
+        for r in range(6):
             finish(r)
         quantise(2, 2)
-        for r in range(8, TILES):
+        for pair in ((8, 9), (10, 11)):
             for a in range(PASSES):
-                multiply(a, r)
-        for r in range(4, TILES):
+                for r in pair:
+                    multiply(a, r)
+        for r in range(6, TILES):
             finish(r)

@@ -53,12 +53,16 @@ def tile_mix_dyq_tm_mul_kernel(tc, dy, w8_words, w8_scales, w4_words, w4_scales,
 
         nc.vector.memset(planes8[:].bitcast(I32), 0)
         nc.vector.memset(plane4[:].bitcast(I32), 0)
-        load_dy(0)
+        staged = keep.tile([P, 2, D], U8, name="staged", align_bytes=64)
         for r in range(4):
-            nc.sync.dma_start(
-                out=planes8[r:P:32, :, :].bitcast(I32),
+            nc.scalar.dma_start(
+                out=staged[r:P:32, :, :].bitcast(I32),
                 in_=w8_scales[:, r:16:4, :].rearrange("a q n -> q a n").bitcast(I32),
             )
+        load_dy(0)
+        for q in range(4):
+            live = slice(32 * q, 32 * q + 4)
+            nc.vector.tensor_copy(out=planes8[live].bitcast(I32), in_=staged[live].bitcast(I32))
         nc.sync.dma_start(out=w8[:].bitcast(I32), in_=w8_words.rearrange("a p n t -> p a (n t)").bitcast(I32))
         load_dy(1)
         load_dy(2)

@@ -66,14 +66,16 @@ def tile_mix_dyq_tm_mul_kernel(tc, dy, w8_words, w8_scales, w4_words, w4_scales,
         nc.sync.dma_start(out=w8[:].bitcast(I32), in_=w8_words.rearrange("a p n t -> p a (n t)").bitcast(I32))
         load_dy(1)
         load_dy(2)
-        for r in range(4):
-            nc.sync.dma_start(out=plane4[r:P:32, :].bitcast(I32), in_=w4_scales[0, r:16:4, :].bitcast(I32))
-        nc.sync.dma_start(out=w4[:].bitcast(I32), in_=w4_words[0].bitcast(I32))
         g_view = g.rearrange("(p r) d -> p r d", r=TILES)
         out_view = out.rearrange("(p r) d -> p r d", r=TILES)
-        for q in range(QUADS):
-            rows = slice(4 * q, 4 * q + 4)
-            nc.sync.dma_start(out=g_sb[:, rows, :], in_=g_view[:, rows, :])
+
+        def load_rest():
+            for r in range(4):
+                nc.scalar.dma_start(out=plane4[r:P:32, :].bitcast(I32), in_=w4_scales[0, r:16:4, :].bitcast(I32))
+            nc.sync.dma_start(out=w4[:].bitcast(I32), in_=w4_words[0].bitcast(I32))
+            for q in range(QUADS):
+                rows = slice(4 * q, 4 * q + 4)
+                nc.sync.dma_start(out=g_sb[:, rows, :], in_=g_view[:, rows, :])
 
         def group(copy, a, q, m0, m1):
             src = raw[a][:].rearrange("p j (m q i) -> p q m j i", q=QUADS, i=4)[:, q]
@@ -110,6 +112,8 @@ def tile_mix_dyq_tm_mul_kernel(tc, dy, w8_words, w8_scales, w4_words, w4_scales,
         for a in range(PASSES - 1):
             group(nc.scalar.copy, a, 2, 0, P)
             group(nc.scalar.copy, a, 1, 0, P)
+            if a == 0:
+                load_rest()
             group(nc.vector.tensor_copy, a, 0, 0, P)
             for q in (0, 2, 1):
                 quantise(a, q)

@@ -16,13 +16,13 @@ P = 128
 K, T, D = 1536, 1536, 512
 PASSES = 3
 TILES = T // P
-QUADS = TILES // 4
+BANKS = 8
 
 FLOPS = 2 * K * T * D
 BYTES = 4 * K * T + 2 * 4 * T * D + 1024 * D + 512 * D // 2 + 48 * D
 
-SPLIT = 32
-STORES = ((0, 3), (3, 6), (6, 8), (8, 10), (10, 12))
+WIDTH = (4, 4, 2)
+QUAD = 4
 
 
 def tile_mix_dyq_tm_mul_kernel(tc, dy, w8_words, w8_scales, w4_words, w4_scales, g, out):
@@ -32,8 +32,7 @@ def tile_mix_dyq_tm_mul_kernel(tc, dy, w8_words, w8_scales, w4_words, w4_scales,
         psum = ctx.enter_context(tc.psum_pool(name="psum", bufs=1))
         ctx.enter_context(tc.manual_schedule())
 
-        planes8 = keep.tile([P, 2, D], U8, name="planes8", align_bytes=64)
-        plane4 = keep.tile([P, D], U8, name="plane4", align_bytes=64)
+        planes = [keep.tile([P, D], U8, name="plane%d" % a, align_bytes=64) for a in range(PASSES)]
         w8 = keep.tile([P, 2, D], U32, name="w8", align_bytes=64)
         w4 = keep.tile([P, 2 * D], U8, name="w4", align_bytes=64)
         raw = [keep.tile([P, 4, T], F32, name="raw%d" % a, align_bytes=64) for a in range(PASSES)]
@@ -43,97 +42,116 @@ def tile_mix_dyq_tm_mul_kernel(tc, dy, w8_words, w8_scales, w4_words, w4_scales,
         codes = {}
         scales = {}
         for a in range(PASSES):
-            for q in range(QUADS):
-                grouped[a, q] = keep.tile([P, 4 * D], BF16, name="grouped%d_%d" % (a, q), align_bytes=64)
-                codes[a, q] = keep.tile([P, D], U32, name="codes%d_%d" % (a, q), align_bytes=64)
-                scales[a, q] = keep.tile([P, D], U8, name="scales%d_%d" % (a, q), align_bytes=64)
+            n = WIDTH[a]
+            for u in range(TILES // n):
+                grouped[a, u] = keep.tile([P, n * D], BF16, name="grouped%d_%d" % (a, u), align_bytes=64)
+                codes[a, u] = keep.tile([P, n * P], U32, name="codes%d_%d" % (a, u), align_bytes=64)
+                scales[a, u] = keep.tile([P, n * P], U8, name="scales%d_%d" % (a, u), align_bytes=64)
+        g_view = g.rearrange("(p r) d -> p r d", r=TILES)
+        out_view = out.rearrange("(p r) d -> p r d", r=TILES)
 
         def load_dy(a):
             nc.sync.dma_start(out=raw[a][:], in_=dy[512 * a : 512 * (a + 1), :].rearrange("(p j) t -> p j t", j=4))
 
-        nc.vector.memset(planes8[:].bitcast(I32), 0)
-        nc.vector.memset(plane4[:].bitcast(I32), 0)
-        staged = keep.tile([P, 2, D], U8, name="staged", align_bytes=64)
-        for r in range(4):
-            nc.scalar.dma_start(
-                out=staged[r:P:32, :, :].bitcast(I32),
-                in_=w8_scales[:, r:16:4, :].rearrange("a q n -> q a n").bitcast(I32),
-            )
-        load_dy(0)
-        for q in range(4):
-            live = slice(32 * q, 32 * q + 4)
-            nc.vector.tensor_copy(out=planes8[live].bitcast(I32), in_=staged[live].bitcast(I32))
-        nc.sync.dma_start(out=w8[:].bitcast(I32), in_=w8_words.rearrange("a p n t -> p a (n t)").bitcast(I32))
-        load_dy(1)
-        load_dy(2)
-        g_view = g.rearrange("(p r) d -> p r d", r=TILES)
-        out_view = out.rearrange("(p r) d -> p r d", r=TILES)
-
-        def load_rest():
+        def load_scale_rows(dst, rows):
             for r in range(4):
-                nc.scalar.dma_start(out=plane4[r:P:32, :].bitcast(I32), in_=w4_scales[0, r:16:4, :].bitcast(I32))
-            nc.sync.dma_start(out=w4[:].bitcast(I32), in_=w4_words[0].bitcast(I32))
-            for q in range(QUADS):
-                rows = slice(4 * q, 4 * q + 4)
-                nc.sync.dma_start(out=g_sb[:, rows, :], in_=g_view[:, rows, :])
+                nc.sync.dma_start(out=dst[r:P:32, :].bitcast(I32), in_=rows[r:16:4, :].bitcast(I32))
 
-        def group(copy, a, q, m0, m1):
-            src = raw[a][:].rearrange("p j (m q i) -> p q m j i", q=QUADS, i=4)[:, q]
-            dst = grouped[a, q][:].rearrange("p (i m j) -> p m j i", i=4, j=4)
-            copy(out=dst[:, m0:m1], in_=src[:, m0:m1])
+        def group(copy, a, u):
+            n = WIDTH[a]
+            src = raw[a][:].rearrange("p j (m u i) -> p u m j i", u=TILES // n, i=n)[:, u]
+            copy(out=grouped[a, u][:].rearrange("p (i m j) -> p m j i", i=n, j=4), in_=src)
 
-        def quantise(a, q):
-            nc.vector.quantize_mx(out=codes[a, q][:].bitcast(E5M2X4), scales=scales[a, q][:], in_=grouped[a, q][:])
+        def quantise(a, u):
+            nc.vector.quantize_mx(out=codes[a, u][:].bitcast(E5M2X4), scales=scales[a, u][:], in_=grouped[a, u][:])
 
         acc = {}
 
         def multiply(a, r):
             if a == 0:
-                acc[r] = psum.tile([P, D], F32, name="acc%d" % (r % 8))
-            cols = slice(P * (r % 4), P * (r % 4 + 1))
+                acc[r] = psum.tile([P, D], F32, name="acc%d" % (r % BANKS))
+            u, i = divmod(r, WIDTH[a])
+            cols = slice(P * i, P * (i + 1))
             nc.tensor.matmul_mx(
                 out=acc[r][:],
-                lhsT=codes[a, r // 4][:, cols].bitcast(E5M2X4),
-                lhsT_scale=scales[a, r // 4][:, cols],
+                lhsT=codes[a, u][:, cols].bitcast(E5M2X4),
+                lhsT_scale=scales[a, u][:, cols],
                 rhs=w8[:, a, :].bitcast(E4M3X4) if a < 2 else w4[:].bitcast(E2M1X4),
-                rhs_scale=planes8[:, a, :] if a < 2 else plane4[:],
+                rhs_scale=planes[a][:],
                 start=(a == 0),
                 stop=(a == PASSES - 1),
             )
 
-        last_of = {hi - 1: lo for lo, hi in STORES}
+        def reopen(r):
+            multiply(0, r + BANKS)
+            multiply(1, r + BANKS)
 
         def finish(r):
             nc.vector.tensor_tensor(out=o_sb[:, r, :], in0=acc[r][:], in1=g_sb[:, r, :], op=MULT)
-            if r in last_of:
-                rows = slice(last_of[r], r + 1)
-                nc.sync.dma_start(out=out_view[:, rows, :], in_=o_sb[:, rows, :])
 
-        for a in range(PASSES - 1):
-            group(nc.scalar.copy, a, 2, 0, P)
-            group(nc.scalar.copy, a, 1, 0, P)
-            if a == 0:
-                load_rest()
-            group(nc.vector.tensor_copy, a, 0, 0, P)
-            for q in (0, 2, 1):
-                quantise(a, q)
-            for r in range(8):
+        def finish_aside(r):
+            sums = keep.tile([P, D], F32, name="sums%d" % r, align_bytes=64)
+            nc.scalar.copy(out=sums[:], in_=acc[r][:])
+            nc.gpsimd.tensor_tensor(out=o_sb[:, r, :], in0=sums[:], in1=g_sb[:, r, :], op=MULT)
+
+        def store(lo):
+            nc.sync.dma_start(out=out_view[:, lo : lo + QUAD, :], in_=o_sb[:, lo : lo + QUAD, :])
+
+        for a in range(PASSES):
+            nc.vector.memset(planes[a][:].bitcast(I32), 0)
+        load_dy(0)
+        load_scale_rows(planes[0], w8_scales[0])
+        nc.sync.dma_start(out=w8[:].bitcast(I32), in_=w8_words.rearrange("a p n t -> p a (n t)").bitcast(I32))
+        load_dy(1)
+        load_scale_rows(planes[1], w8_scales[1])
+        load_dy(2)
+        load_scale_rows(planes[2], w4_scales[0])
+        nc.sync.dma_start(out=w4[:].bitcast(I32), in_=w4_words[0].bitcast(I32))
+        for lo in range(0, TILES, QUAD):
+            nc.sync.dma_start(out=g_sb[:, lo : lo + QUAD, :], in_=g_view[:, lo : lo + QUAD, :])
+
+        for a in range(2):
+            group(nc.scalar.copy, a, 2)
+            group(nc.scalar.copy, a, 1)
+            group(nc.vector.tensor_copy, a, 0)
+            for u in (0, 2, 1):
+                quantise(a, u)
+            for r in range(BANKS):
                 multiply(a, r)
 
-        group(nc.scalar.copy, 2, 1, SPLIT, P)
-        group(nc.scalar.copy, 2, 2, 0, P)
-        group(nc.vector.tensor_copy, 2, 0, 0, P)
-        group(nc.vector.tensor_copy, 2, 1, 0, SPLIT)
-        quantise(2, 0)
-        quantise(2, 1)
-        for r in range(8):
-            multiply(2, r)
+        for u in (2, 3):
+            group(nc.scalar.copy, 2, u)
+        for u in (0, 1):
+            group(nc.vector.tensor_copy, 2, u)
+        for u in (0, 1, 2):
+            quantise(2, u)
         for r in range(6):
+            multiply(2, r)
+
+        finish_aside(0)
+        reopen(0)
+        group(nc.scalar.copy, 2, 4)
+        for r in (1, 2, 3):
             finish(r)
-        quantise(2, 2)
-        for pair in ((8, 9), (10, 11)):
-            for a in range(PASSES):
-                for r in pair:
-                    multiply(a, r)
-        for r in range(6, TILES):
+        store(0)
+        reopen(1)
+        reopen(2)
+        quantise(2, 3)
+        quantise(2, 4)
+        for r in (6, 7, 8, 9):
+            multiply(2, r)
+        reopen(3)
+
+        finish_aside(4)
+        group(nc.scalar.copy, 2, 5)
+        for r in (5, 6, 7):
             finish(r)
+        store(4)
+        quantise(2, 5)
+        for r in (10, 11):
+            multiply(2, r)
+
+        finish_aside(8)
+        for r in (9, 10, 11):
+            finish(r)
+        store(8)

@@ -14,15 +14,14 @@ MULT = mybir.AluOpType.mult
 
 P = 128
 K, T, D = 1536, 1536, 512
-PASSES = 3
 TILES = T // P
 BANKS = 8
+FIRST, MIDDLE, LAST = 2, 0, 1
+WIDTH = {FIRST: 4, MIDDLE: 4, LAST: 2}
+QUAD = 4
 
 FLOPS = 2 * K * T * D
 BYTES = 4 * K * T + 2 * 4 * T * D + 1024 * D + 512 * D // 2 + 48 * D
-
-WIDTH = (4, 4, 2)
-QUAD = 4
 
 
 def tile_mix_dyq_tm_mul_kernel(tc, dy, w8_words, w8_scales, w4_words, w4_scales, g, out):
@@ -32,30 +31,24 @@ def tile_mix_dyq_tm_mul_kernel(tc, dy, w8_words, w8_scales, w4_words, w4_scales,
         psum = ctx.enter_context(tc.psum_pool(name="psum", bufs=1))
         ctx.enter_context(tc.manual_schedule())
 
-        planes = [keep.tile([P, D], U8, name="plane%d" % a, align_bytes=64) for a in range(PASSES)]
-        w8 = keep.tile([P, 2, D], U32, name="w8", align_bytes=64)
-        w4 = keep.tile([P, 2 * D], U8, name="w4", align_bytes=64)
-        raw = [keep.tile([P, 4, T], F32, name="raw%d" % a, align_bytes=64) for a in range(PASSES)]
+        word_rows = [w8_words[a].rearrange("p n t -> p (n t)") for a in range(2)] + [w4_words[0]]
+        scale_rows = [w8_scales[0], w8_scales[1], w4_scales[0]]
+        formats = [E4M3X4, E4M3X4, E2M1X4]
+        g_view = g.rearrange("(p r) d -> p r d", r=TILES)
+        out_view = out.rearrange("(p r) d -> p r d", r=TILES)
+
         g_sb = keep.tile([P, TILES, D], F32, name="g_sb", align_bytes=64)
         o_sb = keep.tile([P, TILES, D], F32, name="o_sb", align_bytes=64)
-        grouped = {}
-        codes = {}
-        scales = {}
-        for a in range(PASSES):
+        raw, words, planes, grouped, codes, scales = {}, {}, {}, {}, {}, {}
+        for a in (FIRST, MIDDLE, LAST):
+            raw[a] = keep.tile([P, 4, T], F32, name="raw%d" % a, align_bytes=64)
+            words[a] = keep.tile([P, word_rows[a].shape[1]], U8, name="words%d" % a, align_bytes=64)
+            planes[a] = keep.tile([P, D], U8, name="plane%d" % a, align_bytes=64)
             n = WIDTH[a]
             for u in range(TILES // n):
                 grouped[a, u] = keep.tile([P, n * D], BF16, name="grouped%d_%d" % (a, u), align_bytes=64)
                 codes[a, u] = keep.tile([P, n * P], U32, name="codes%d_%d" % (a, u), align_bytes=64)
                 scales[a, u] = keep.tile([P, n * P], U8, name="scales%d_%d" % (a, u), align_bytes=64)
-        g_view = g.rearrange("(p r) d -> p r d", r=TILES)
-        out_view = out.rearrange("(p r) d -> p r d", r=TILES)
-
-        def load_dy(a):
-            nc.sync.dma_start(out=raw[a][:], in_=dy[512 * a : 512 * (a + 1), :].rearrange("(p j) t -> p j t", j=4))
-
-        def load_scale_rows(dst, rows):
-            for r in range(4):
-                nc.sync.dma_start(out=dst[r:P:32, :].bitcast(I32), in_=rows[r:16:4, :].bitcast(I32))
 
         def group(copy, a, u):
             n = WIDTH[a]
@@ -68,7 +61,7 @@ def tile_mix_dyq_tm_mul_kernel(tc, dy, w8_words, w8_scales, w4_words, w4_scales,
         acc = {}
 
         def multiply(a, r):
-            if a == 0:
+            if a == FIRST:
                 acc[r] = psum.tile([P, D], F32, name="acc%d" % (r % BANKS))
             u, i = divmod(r, WIDTH[a])
             cols = slice(P * i, P * (i + 1))
@@ -76,15 +69,15 @@ def tile_mix_dyq_tm_mul_kernel(tc, dy, w8_words, w8_scales, w4_words, w4_scales,
                 out=acc[r][:],
                 lhsT=codes[a, u][:, cols].bitcast(E5M2X4),
                 lhsT_scale=scales[a, u][:, cols],
-                rhs=w8[:, a, :].bitcast(E4M3X4) if a < 2 else w4[:].bitcast(E2M1X4),
+                rhs=words[a][:].bitcast(formats[a]),
                 rhs_scale=planes[a][:],
-                start=(a == 0),
-                stop=(a == PASSES - 1),
+                start=(a == FIRST),
+                stop=(a == LAST),
             )
 
         def reopen(r):
-            multiply(0, r + BANKS)
-            multiply(1, r + BANKS)
+            multiply(FIRST, r + BANKS)
+            multiply(MIDDLE, r + BANKS)
 
         def finish(r):
             nc.vector.tensor_tensor(out=o_sb[:, r, :], in0=acc[r][:], in1=g_sb[:, r, :], op=MULT)
@@ -97,20 +90,25 @@ def tile_mix_dyq_tm_mul_kernel(tc, dy, w8_words, w8_scales, w4_words, w4_scales,
         def store(lo):
             nc.sync.dma_start(out=out_view[:, lo : lo + QUAD, :], in_=o_sb[:, lo : lo + QUAD, :])
 
-        for a in range(PASSES):
+        def load_scale_rows(queue, dst, a):
+            for r in range(4):
+                queue.dma_start(out=dst[r:P:32, :].bitcast(I32), in_=scale_rows[a][r:16:4, :].bitcast(I32))
+
+        staged = keep.tile([P, D], U8, name="staged", align_bytes=64)
+        load_scale_rows(nc.scalar, staged, FIRST)
+        for a in (FIRST, MIDDLE, LAST):
             nc.vector.memset(planes[a][:].bitcast(I32), 0)
-        load_dy(0)
-        load_scale_rows(planes[0], w8_scales[0])
-        nc.sync.dma_start(out=w8[:].bitcast(I32), in_=w8_words.rearrange("a p n t -> p a (n t)").bitcast(I32))
-        load_dy(1)
-        load_scale_rows(planes[1], w8_scales[1])
-        load_dy(2)
-        load_scale_rows(planes[2], w4_scales[0])
-        nc.sync.dma_start(out=w4[:].bitcast(I32), in_=w4_words[0].bitcast(I32))
+            nc.sync.dma_start(out=raw[a][:], in_=dy[512 * a : 512 * (a + 1), :].rearrange("(p j) t -> p j t", j=4))
+            nc.sync.dma_start(out=words[a][:].bitcast(I32), in_=word_rows[a].bitcast(I32))
+            if a != FIRST:
+                load_scale_rows(nc.sync, planes[a], a)
+        for q in range(4):
+            live = slice(32 * q, 32 * q + 4)
+            nc.vector.tensor_copy(out=planes[FIRST][live].bitcast(I32), in_=staged[live].bitcast(I32))
         for lo in range(0, TILES, QUAD):
             nc.sync.dma_start(out=g_sb[:, lo : lo + QUAD, :], in_=g_view[:, lo : lo + QUAD, :])
 
-        for a in range(2):
+        for a in (FIRST, MIDDLE):
             group(nc.scalar.copy, a, 2)
             group(nc.scalar.copy, a, 1)
             group(nc.vector.tensor_copy, a, 0)
@@ -120,36 +118,33 @@ def tile_mix_dyq_tm_mul_kernel(tc, dy, w8_words, w8_scales, w4_words, w4_scales,
                 multiply(a, r)
 
         for u in (2, 3):
-            group(nc.scalar.copy, 2, u)
+            group(nc.scalar.copy, LAST, u)
         for u in (0, 1):
-            group(nc.vector.tensor_copy, 2, u)
-        for u in (0, 1, 2):
-            quantise(2, u)
-        for r in range(6):
-            multiply(2, r)
+            group(nc.vector.tensor_copy, LAST, u)
+        for u in range(4):
+            quantise(LAST, u)
+        for r in range(BANKS):
+            multiply(LAST, r)
 
         finish_aside(0)
         reopen(0)
-        group(nc.scalar.copy, 2, 4)
+        group(nc.scalar.copy, LAST, 4)
         for r in (1, 2, 3):
             finish(r)
+            reopen(r)
         store(0)
-        reopen(1)
-        reopen(2)
-        quantise(2, 3)
-        quantise(2, 4)
-        for r in (6, 7, 8, 9):
-            multiply(2, r)
-        reopen(3)
+        quantise(LAST, 4)
+        for r in (8, 9):
+            multiply(LAST, r)
 
         finish_aside(4)
-        group(nc.scalar.copy, 2, 5)
+        group(nc.scalar.copy, LAST, 5)
         for r in (5, 6, 7):
             finish(r)
         store(4)
-        quantise(2, 5)
+        quantise(LAST, 5)
         for r in (10, 11):
-            multiply(2, r)
+            multiply(LAST, r)
 
         finish_aside(8)
         for r in (9, 10, 11):

@@ -37,18 +37,18 @@ def tile_mix_dyq_tm_mul_kernel(tc, dy, w8_words, w8_scales, w4_words, w4_scales,
         g_view = g.rearrange("(p r) d -> p r d", r=TILES)
         out_view = out.rearrange("(p r) d -> p r d", r=TILES)
 
-        g_sb = keep.tile([P, TILES, D], F32, name="g_sb", align_bytes=64)
-        o_sb = keep.tile([P, TILES, D], F32, name="o_sb", align_bytes=64)
+        g_sb = keep.tile([P, TILES, D], F32, name="g_sb", align_bytes=256)
+        o_sb = keep.tile([P, TILES, D], F32, name="o_sb", align_bytes=256)
         raw, words, planes, grouped, codes, scales = {}, {}, {}, {}, {}, {}
         for a in (FIRST, MIDDLE, LAST):
-            raw[a] = keep.tile([P, 4, T], F32, name="raw%d" % a, align_bytes=64)
-            words[a] = keep.tile([P, word_rows[a].shape[1]], U8, name="words%d" % a, align_bytes=64)
-            planes[a] = keep.tile([P, D], U8, name="plane%d" % a, align_bytes=64)
+            raw[a] = keep.tile([P, 4, T], F32, name="raw%d" % a, align_bytes=256)
+            words[a] = keep.tile([P, word_rows[a].shape[1]], U8, name="words%d" % a, align_bytes=256)
+            planes[a] = keep.tile([P, D], U8, name="plane%d" % a, align_bytes=256)
             n = WIDTH[a]
             for u in range(TILES // n):
-                grouped[a, u] = keep.tile([P, n * D], BF16, name="grouped%d_%d" % (a, u), align_bytes=64)
-                codes[a, u] = keep.tile([P, n * P], U32, name="codes%d_%d" % (a, u), align_bytes=64)
-                scales[a, u] = keep.tile([P, n * P], U8, name="scales%d_%d" % (a, u), align_bytes=64)
+                grouped[a, u] = keep.tile([P, n * D], BF16, name="grouped%d_%d" % (a, u), align_bytes=256)
+                codes[a, u] = keep.tile([P, n * P], U32, name="codes%d_%d" % (a, u), align_bytes=256)
+                scales[a, u] = keep.tile([P, n * P], U8, name="scales%d_%d" % (a, u), align_bytes=256)
 
         def group(copy, a, u):
             n = WIDTH[a]
@@ -83,7 +83,7 @@ def tile_mix_dyq_tm_mul_kernel(tc, dy, w8_words, w8_scales, w4_words, w4_scales,
             nc.vector.tensor_tensor(out=o_sb[:, r, :], in0=acc[r][:], in1=g_sb[:, r, :], op=MULT)
 
         def finish_aside(r):
-            sums = keep.tile([P, D], F32, name="sums%d" % r, align_bytes=64)
+            sums = keep.tile([P, D], F32, name="sums%d" % r, align_bytes=256)
             nc.scalar.copy(out=sums[:], in_=acc[r][:])
             nc.gpsimd.tensor_tensor(out=o_sb[:, r, :], in0=sums[:], in1=g_sb[:, r, :], op=MULT)
 
@@ -94,7 +94,7 @@ def tile_mix_dyq_tm_mul_kernel(tc, dy, w8_words, w8_scales, w4_words, w4_scales,
             for r in range(4):
                 queue.dma_start(out=dst[r:P:32, :].bitcast(I32), in_=scale_rows[a][r:16:4, :].bitcast(I32))
 
-        staged = keep.tile([P, D], U8, name="staged", align_bytes=64)
+        staged = keep.tile([P, D], U8, name="staged", align_bytes=256)
         load_scale_rows(nc.scalar, staged, FIRST)
         for a in (FIRST, MIDDLE, LAST):
             nc.vector.memset(planes[a][:].bitcast(I32), 0)

@@ -16,47 +16,50 @@ P = 128
 K, T, D = 1536, 1536, 512
 TILES = T // P
 BANKS = 8
-FIRST, MIDDLE, LAST = 2, 0, 1
-WIDTH = {FIRST: 4, MIDDLE: 4, LAST: 2}
-QUAD = 4
-
 FLOPS = 2 * K * T * D
 BYTES = 4 * K * T + 2 * 4 * T * D + 1024 * D + 512 * D // 2 + 48 * D
+FIRST, MIDDLE, LAST = 2, 0, 1
+WIDTH = [4, 2, 4]
+QUAD = 4
 
 
 def tile_mix_dyq_tm_mul_kernel(tc, dy, w8_words, w8_scales, w4_words, w4_scales, g, out):
     nc = tc.nc
     with ExitStack() as ctx:
         keep = ctx.enter_context(tc.tile_pool(name="keep", bufs=1))
+        rows = ctx.enter_context(tc.tile_pool(name="rows", bufs=2))
         psum = ctx.enter_context(tc.psum_pool(name="psum", bufs=1))
         ctx.enter_context(tc.manual_schedule())
 
-        word_rows = [w8_words[a].rearrange("p n t -> p (n t)") for a in range(2)] + [w4_words[0]]
-        scale_rows = [w8_scales[0], w8_scales[1], w4_scales[0]]
-        formats = [E4M3X4, E4M3X4, E2M1X4]
         g_view = g.rearrange("(p r) d -> p r d", r=TILES)
         out_view = out.rearrange("(p r) d -> p r d", r=TILES)
 
-        g_sb = keep.tile([P, TILES, D], F32, name="g_sb", align_bytes=256)
         o_sb = keep.tile([P, TILES, D], F32, name="o_sb", align_bytes=256)
-        raw, words, planes, grouped, codes, scales = {}, {}, {}, {}, {}, {}
-        for a in (FIRST, MIDDLE, LAST):
-            raw[a] = keep.tile([P, 4, T], F32, name="raw%d" % a, align_bytes=256)
-            words[a] = keep.tile([P, word_rows[a].shape[1]], U8, name="words%d" % a, align_bytes=256)
-            planes[a] = keep.tile([P, D], U8, name="plane%d" % a, align_bytes=256)
+        word_rows = [w8_words[a].rearrange("p n t -> p (n t)") for a in range(2)] + [w4_words[0]]
+        scale_rows = [w8_scales[0], w8_scales[1], w4_scales[0]]
+        formats = [E4M3X4, E4M3X4, E2M1X4]
+        words = [keep.tile([P, word_rows[a].shape[1]], U8, name="words%d" % a, align_bytes=256) for a in range(3)]
+        planes = [keep.tile([P, D], U8, name="plane%d" % a, align_bytes=256) for a in range(3)]
+        staged = keep.tile([P, D], U8, name="staged", align_bytes=256)
+        early = keep.tile([P, 2, QUAD * D], BF16, name="early", align_bytes=256)
+        raw, g_sb, grouped, codes, scales = {}, {}, {}, {}, {}
+        for a in range(3):
             n = WIDTH[a]
             for u in range(TILES // n):
-                grouped[a, u] = keep.tile([P, n * D], BF16, name="grouped%d_%d" % (a, u), align_bytes=256)
+                if a == MIDDLE and u != 1:
+                    grouped[a, u] = early[:, u // 2, :]
+                else:
+                    grouped[a, u] = keep.tile([P, n * D], BF16, name="grouped%d_%d" % (a, u), align_bytes=256)[:, :]
                 codes[a, u] = keep.tile([P, n * P], U32, name="codes%d_%d" % (a, u), align_bytes=256)
                 scales[a, u] = keep.tile([P, n * P], U8, name="scales%d_%d" % (a, u), align_bytes=256)
 
-        def group(copy, a, u):
+        def group(copy, a, u, m=slice(0, P)):
             n = WIDTH[a]
-            src = raw[a][:].rearrange("p j (m u i) -> p u m j i", u=TILES // n, i=n)[:, u]
-            copy(out=grouped[a, u][:].rearrange("p (i m j) -> p m j i", i=n, j=4), in_=src)
+            src = raw[a][:].rearrange("p (j m u i) -> p u m j i", j=4, u=TILES // n, i=n)[:, u]
+            copy(out=grouped[a, u].rearrange("p (i m j) -> p m j i", i=n, j=4)[:, m], in_=src[:, m])
 
         def quantise(a, u):
-            nc.vector.quantize_mx(out=codes[a, u][:].bitcast(E5M2X4), scales=scales[a, u][:], in_=grouped[a, u][:])
+            nc.vector.quantize_mx(out=codes[a, u][:].bitcast(E5M2X4), scales=scales[a, u][:], in_=grouped[a, u])
 
         acc = {}
 
@@ -80,42 +83,63 @@ def tile_mix_dyq_tm_mul_kernel(tc, dy, w8_words, w8_scales, w4_words, w4_scales,
             multiply(MIDDLE, r + BANKS)
 
         def finish(r):
-            nc.vector.tensor_tensor(out=o_sb[:, r, :], in0=acc[r][:], in1=g_sb[:, r, :], op=MULT)
+            nc.vector.tensor_tensor(out=o_sb[:, r, :], in0=acc[r][:], in1=g_sb[r // QUAD][:, r % QUAD, :], op=MULT)
 
         def finish_aside(r):
             sums = keep.tile([P, D], F32, name="sums%d" % r, align_bytes=256)
             nc.scalar.copy(out=sums[:], in_=acc[r][:])
-            nc.gpsimd.tensor_tensor(out=o_sb[:, r, :], in0=sums[:], in1=g_sb[:, r, :], op=MULT)
+            nc.gpsimd.tensor_tensor(out=o_sb[:, r, :], in0=sums[:], in1=g_sb[r // QUAD][:, r % QUAD, :], op=MULT)
 
         def store(lo):
             nc.sync.dma_start(out=out_view[:, lo : lo + QUAD, :], in_=o_sb[:, lo : lo + QUAD, :])
 
-        def load_scale_rows(queue, dst, a):
-            for r in range(4):
+        def load_pass(a):
+            raw[a] = rows.tile([P, 4 * T], F32, name="raw", align_bytes=256)
+            nc.sync.dma_start(out=raw[a][:], in_=dy[512 * a : 512 * (a + 1), :].rearrange("(p j) t -> p (j t)", j=4))
+            nc.sync.dma_start(out=words[a][:].bitcast(I32), in_=word_rows[a].bitcast(I32))
+
+        def load_scale_rows(queue, dst, a, which):
+            for r in which:
                 queue.dma_start(out=dst[r:P:32, :].bitcast(I32), in_=scale_rows[a][r:16:4, :].bitcast(I32))
 
-        staged = keep.tile([P, D], U8, name="staged", align_bytes=256)
-        load_scale_rows(nc.scalar, staged, FIRST)
-        for a in (FIRST, MIDDLE, LAST):
+        def load_g(n, name):
+            g_sb[n] = keep.tile([P, QUAD, D], F32, name=name, align_bytes=256)
+            nc.sync.dma_start(out=g_sb[n][:], in_=g_view[:, QUAD * n : QUAD * (n + 1), :])
+
+        load_scale_rows(nc.scalar, staged, FIRST, range(4))
+        for a in (MIDDLE, LAST, FIRST):
             nc.vector.memset(planes[a][:].bitcast(I32), 0)
-            nc.sync.dma_start(out=raw[a][:], in_=dy[512 * a : 512 * (a + 1), :].rearrange("(p j) t -> p j t", j=4))
-            nc.sync.dma_start(out=words[a][:].bitcast(I32), in_=word_rows[a].bitcast(I32))
-            if a != FIRST:
-                load_scale_rows(nc.sync, planes[a], a)
+        load_pass(FIRST)
+        load_scale_rows(nc.sync, planes[MIDDLE], MIDDLE, range(1))
+        load_pass(MIDDLE)
         for q in range(4):
             live = slice(32 * q, 32 * q + 4)
             nc.vector.tensor_copy(out=planes[FIRST][live].bitcast(I32), in_=staged[live].bitcast(I32))
-        for lo in range(0, TILES, QUAD):
-            nc.sync.dma_start(out=g_sb[:, lo : lo + QUAD, :], in_=g_view[:, lo : lo + QUAD, :])
 
-        for a in (FIRST, MIDDLE):
-            group(nc.scalar.copy, a, 2)
-            group(nc.scalar.copy, a, 1)
-            group(nc.vector.tensor_copy, a, 0)
-            for u in (0, 2, 1):
-                quantise(a, u)
-            for r in range(BANKS):
-                multiply(a, r)
+        group(nc.scalar.copy, FIRST, 2, slice(0, P // 2))
+        load_scale_rows(nc.scalar, planes[MIDDLE], MIDDLE, range(1, 4))
+        group(nc.scalar.copy, FIRST, 2, slice(P // 2, P))
+        for u in (0, 1):
+            group(nc.vector.tensor_copy, FIRST, u)
+        load_pass(LAST)
+        for u in range(3):
+            quantise(FIRST, u)
+        for r in range(BANKS):
+            multiply(FIRST, r)
+
+        group(nc.scalar.copy, MIDDLE, 2, slice(0, P // 2))
+        load_scale_rows(nc.scalar, planes[LAST], LAST, range(4))
+        group(nc.scalar.copy, MIDDLE, 2, slice(P // 2, P))
+        group(nc.scalar.copy, MIDDLE, 1)
+        group(nc.vector.tensor_copy, MIDDLE, 0)
+        for u in (0, 2):
+            quantise(MIDDLE, u)
+        load_g(0, "early")
+        load_g(1, "g1")
+        load_g(2, "g2")
+        quantise(MIDDLE, 1)
+        for r in range(BANKS):
+            multiply(MIDDLE, r)
 
         for u in (2, 3):
             group(nc.scalar.copy, LAST, u)

@@ -18,159 +18,152 @@ TILES = T // P
 BANKS = 8
 FLOPS = 2 * K * T * D
 BYTES = 4 * K * T + 2 * 4 * T * D + 1024 * D + 512 * D // 2 + 48 * D
-FIRST, MIDDLE, LAST = 2, 0, 1
-WIDTH = [4, 2, 4]
-QUAD = 4
+WIDTH = [4, 4, 2]
+BANK = [0, 1, 2, 3, 4, 5, 6, 7, 0, 1, 2, 3]
+SPLIT = 384
+HALF = TILES // 2
 
 
 def tile_mix_dyq_tm_mul_kernel(tc, dy, w8_words, w8_scales, w4_words, w4_scales, g, out):
     nc = tc.nc
     with ExitStack() as ctx:
         keep = ctx.enter_context(tc.tile_pool(name="keep", bufs=1))
-        rows = ctx.enter_context(tc.tile_pool(name="rows", bufs=2))
         psum = ctx.enter_context(tc.psum_pool(name="psum", bufs=1))
         ctx.enter_context(tc.manual_schedule())
 
         g_view = g.rearrange("(p r) d -> p r d", r=TILES)
         out_view = out.rearrange("(p r) d -> p r d", r=TILES)
 
-        o_sb = keep.tile([P, TILES, D], F32, name="o_sb", align_bytes=256)
-        word_rows = [w8_words[a].rearrange("p n t -> p (n t)") for a in range(2)] + [w4_words[0]]
-        scale_rows = [w8_scales[0], w8_scales[1], w4_scales[0]]
-        formats = [E4M3X4, E4M3X4, E2M1X4]
-        words = [keep.tile([P, word_rows[a].shape[1]], U8, name="words%d" % a, align_bytes=256) for a in range(3)]
-        planes = [keep.tile([P, D], U8, name="plane%d" % a, align_bytes=256) for a in range(3)]
-        staged = keep.tile([P, D], U8, name="staged", align_bytes=256)
-        early = keep.tile([P, 2, QUAD * D], BF16, name="early", align_bytes=256)
-        raw, g_sb, grouped, codes, scales = {}, {}, {}, {}, {}
+        raw8 = keep.tile([P, 2, 4 * T], F32, name="raw8", align_bytes=256)
+        raw4 = keep.tile([P, 4 * T], F32, name="raw4", align_bytes=256)
+        words8 = keep.tile([P, 2, 4 * D], U8, name="words8", align_bytes=256)
+        words4 = keep.tile([P, 2 * D], U8, name="words4", align_bytes=256)
+        plane8 = keep.tile([P, 2, D], U8, name="plane8", align_bytes=256)
+        plane4 = keep.tile([P, D], U8, name="plane4", align_bytes=256)
+        g_sb = [keep.tile([P, HALF, D], F32, name="g%d" % h, align_bytes=256) for h in range(2)]
+        o_sb = [keep.tile([P, HALF, D], F32, name="o%d" % h, align_bytes=256) for h in range(2)]
+        raw = [raw8[:, 0, :], raw8[:, 1, :], raw4[:, :]]
+        words = [words8[:, 0, :].bitcast(E4M3X4), words8[:, 1, :].bitcast(E4M3X4), words4[:, :].bitcast(E2M1X4)]
+        planes = [plane8[:, 0, :], plane8[:, 1, :], plane4[:, :]]
+        grouped, codes, scales, acc, sums = {}, {}, {}, {}, {}
         for a in range(3):
             n = WIDTH[a]
             for u in range(TILES // n):
-                if a == MIDDLE and u != 1:
-                    grouped[a, u] = early[:, u // 2, :]
-                else:
-                    grouped[a, u] = keep.tile([P, n * D], BF16, name="grouped%d_%d" % (a, u), align_bytes=256)[:, :]
+                grouped[a, u] = keep.tile([P, n * D], BF16, name="grouped%d_%d" % (a, u), align_bytes=256)
                 codes[a, u] = keep.tile([P, n * P], U32, name="codes%d_%d" % (a, u), align_bytes=256)
                 scales[a, u] = keep.tile([P, n * P], U8, name="scales%d_%d" % (a, u), align_bytes=256)
 
-        def group(copy, a, u, m=slice(0, P)):
+        def group(copy, a, u):
             n = WIDTH[a]
-            src = raw[a][:].rearrange("p (j m u i) -> p u m j i", j=4, u=TILES // n, i=n)[:, u]
-            copy(out=grouped[a, u].rearrange("p (i m j) -> p m j i", i=n, j=4)[:, m], in_=src[:, m])
+            src = raw[a].rearrange("p (j m u i) -> p u m j i", j=4, u=TILES // n, i=n)[:, u]
+            copy(out=grouped[a, u][:].rearrange("p (i m j) -> p m j i", i=n, j=4), in_=src)
 
         def quantise(a, u):
-            nc.vector.quantize_mx(out=codes[a, u][:].bitcast(E5M2X4), scales=scales[a, u][:], in_=grouped[a, u])
-
-        acc = {}
+            nc.vector.quantize_mx(out=codes[a, u][:].bitcast(E5M2X4), scales=scales[a, u][:], in_=grouped[a, u][:])
 
         def multiply(a, r):
-            if a == FIRST:
-                acc[r] = psum.tile([P, D], F32, name="acc%d" % (r % BANKS))
+            if a == 0:
+                acc[r] = psum.tile([P, D], F32, name="acc%d" % BANK[r])
             u, i = divmod(r, WIDTH[a])
             cols = slice(P * i, P * (i + 1))
             nc.tensor.matmul_mx(
                 out=acc[r][:],
                 lhsT=codes[a, u][:, cols].bitcast(E5M2X4),
                 lhsT_scale=scales[a, u][:, cols],
-                rhs=words[a][:].bitcast(formats[a]),
-                rhs_scale=planes[a][:],
-                start=(a == FIRST),
-                stop=(a == LAST),
+                rhs=words[a],
+                rhs_scale=planes[a],
+                start=(a == 0),
+                stop=(a == 2),
             )
 
         def reopen(r):
-            multiply(FIRST, r + BANKS)
-            multiply(MIDDLE, r + BANKS)
+            for a in range(2):
+                multiply(a, r)
 
-        def finish(r):
-            nc.vector.tensor_tensor(out=o_sb[:, r, :], in0=acc[r][:], in1=g_sb[r // QUAD][:, r % QUAD, :], op=MULT)
+        def finish(r, cols=slice(0, D)):
+            h, i = divmod(r, HALF)
+            nc.vector.tensor_tensor(out=o_sb[h][:, i, cols], in0=acc[r][:, cols], in1=g_sb[h][:, i, cols], op=MULT)
 
-        def finish_aside(r):
-            sums = keep.tile([P, D], F32, name="sums%d" % r, align_bytes=256)
-            nc.scalar.copy(out=sums[:], in_=acc[r][:])
-            nc.gpsimd.tensor_tensor(out=o_sb[:, r, :], in0=sums[:], in1=g_sb[r // QUAD][:, r % QUAD, :], op=MULT)
+        def set_aside(r, cols=slice(0, D)):
+            sums[r] = keep.tile([P, D], F32, name="sums%d" % r, align_bytes=256)
+            nc.scalar.copy(out=sums[r][:, cols], in_=acc[r][:, cols])
 
-        def store(lo):
-            nc.sync.dma_start(out=out_view[:, lo : lo + QUAD, :], in_=o_sb[:, lo : lo + QUAD, :])
+        def finish_aside(r, cols=slice(0, D)):
+            h, i = divmod(r, HALF)
+            nc.gpsimd.tensor_tensor(out=o_sb[h][:, i, cols], in0=sums[r][:, cols], in1=g_sb[h][:, i, cols], op=MULT)
 
-        def load_pass(a):
-            raw[a] = rows.tile([P, 4 * T], F32, name="raw", align_bytes=256)
-            nc.sync.dma_start(out=raw[a][:], in_=dy[512 * a : 512 * (a + 1), :].rearrange("(p j) t -> p (j t)", j=4))
-            nc.sync.dma_start(out=words[a][:].bitcast(I32), in_=word_rows[a].bitcast(I32))
+        left, right = slice(0, SPLIT), slice(SPLIT, D)
 
-        def load_scale_rows(queue, dst, a, which):
-            for r in which:
-                queue.dma_start(out=dst[r:P:32, :].bitcast(I32), in_=scale_rows[a][r:16:4, :].bitcast(I32))
+        def half(h):
+            return slice(HALF * h, HALF * (h + 1))
 
-        def load_g(n, name):
-            g_sb[n] = keep.tile([P, QUAD, D], F32, name=name, align_bytes=256)
-            nc.sync.dma_start(out=g_sb[n][:], in_=g_view[:, QUAD * n : QUAD * (n + 1), :])
+        nc.vector.memset(plane8[:].bitcast(I32), 0)
+        nc.vector.memset(plane4[:].bitcast(I32), 0)
+        nc.sync.dma_start(out=raw8[:], in_=dy[0:1024, :].rearrange("(a p j) t -> p a (j t)", a=2, j=4))
+        nc.sync.dma_start(out=words8[:].bitcast(I32), in_=w8_words.rearrange("a p n t -> p a (n t)").bitcast(I32))
+        for r in range(4):
+            nc.sync.dma_start(
+                out=plane8[r:P:32, :, :].bitcast(I32), in_=w8_scales[:, r:16:4, :].rearrange("a q n -> q a n").bitcast(I32)
+            )
+        nc.sync.dma_start(out=raw4[:], in_=dy[1024:K, :].rearrange("(p j) t -> p (j t)", j=4))
+        nc.sync.dma_start(out=words4[:].bitcast(I32), in_=w4_words[0].bitcast(I32))
+        for r in range(4):
+            nc.sync.dma_start(out=plane4[r:P:32, :].bitcast(I32), in_=w4_scales[0][r:16:4, :].bitcast(I32))
+        for h in range(2):
+            nc.sync.dma_start(out=g_sb[h][:], in_=g_view[:, half(h), :])
 
-        load_scale_rows(nc.scalar, staged, FIRST, range(4))
-        for a in (MIDDLE, LAST, FIRST):
-            nc.vector.memset(planes[a][:].bitcast(I32), 0)
-        load_pass(FIRST)
-        load_scale_rows(nc.sync, planes[MIDDLE], MIDDLE, range(1))
-        load_pass(MIDDLE)
-        for q in range(4):
-            live = slice(32 * q, 32 * q + 4)
-            nc.vector.tensor_copy(out=planes[FIRST][live].bitcast(I32), in_=staged[live].bitcast(I32))
+        group(nc.scalar.copy, 0, 1)
+        group(nc.scalar.copy, 1, 1)
+        group(nc.scalar.copy, 1, 2)
+        group(nc.vector.tensor_copy, 0, 0)
+        group(nc.vector.tensor_copy, 1, 0)
+        quantise(0, 0)
+        quantise(1, 0)
+        group(nc.vector.tensor_copy, 0, 2)
+        quantise(0, 1)
+        quantise(1, 1)
+        quantise(0, 2)
+        quantise(1, 2)
+        for quad in range(2):
+            for a in range(2):
+                for r in range(4 * quad, 4 * quad + 4):
+                    multiply(a, r)
 
-        group(nc.scalar.copy, FIRST, 2, slice(0, P // 2))
-        load_scale_rows(nc.scalar, planes[MIDDLE], MIDDLE, range(1, 4))
-        group(nc.scalar.copy, FIRST, 2, slice(P // 2, P))
-        for u in (0, 1):
-            group(nc.vector.tensor_copy, FIRST, u)
-        load_pass(LAST)
-        for u in range(3):
-            quantise(FIRST, u)
-        for r in range(BANKS):
-            multiply(FIRST, r)
-
-        group(nc.scalar.copy, MIDDLE, 2, slice(0, P // 2))
-        load_scale_rows(nc.scalar, planes[LAST], LAST, range(4))
-        group(nc.scalar.copy, MIDDLE, 2, slice(P // 2, P))
-        group(nc.scalar.copy, MIDDLE, 1)
-        group(nc.vector.tensor_copy, MIDDLE, 0)
-        for u in (0, 2):
-            quantise(MIDDLE, u)
-        load_g(0, "early")
-        load_g(1, "g1")
-        load_g(2, "g2")
-        quantise(MIDDLE, 1)
-        for r in range(BANKS):
-            multiply(MIDDLE, r)
-
+        group(nc.scalar.copy, 2, 2)
+        group(nc.scalar.copy, 2, 4)
+        group(nc.vector.tensor_copy, 2, 0)
+        group(nc.vector.tensor_copy, 2, 1)
+        quantise(2, 0)
+        quantise(2, 1)
+        group(nc.vector.tensor_copy, 2, 3)
         for u in (2, 3):
-            group(nc.scalar.copy, LAST, u)
-        for u in (0, 1):
-            group(nc.vector.tensor_copy, LAST, u)
-        for u in range(4):
-            quantise(LAST, u)
+            quantise(2, u)
         for r in range(BANKS):
-            multiply(LAST, r)
+            multiply(2, r)
 
+        set_aside(0)
+        set_aside(1, left)
+        group(nc.scalar.copy, 2, 5)
+        reopen(8)
+        set_aside(6)
+        set_aside(7, left)
         finish_aside(0)
-        reopen(0)
-        group(nc.scalar.copy, LAST, 4)
-        for r in (1, 2, 3):
+        finish_aside(1, left)
+        finish(1, right)
+        reopen(9)
+        for r in (2, 3):
             finish(r)
-            reopen(r)
-        store(0)
-        quantise(LAST, 4)
-        for r in (8, 9):
-            multiply(LAST, r)
-
-        finish_aside(4)
-        group(nc.scalar.copy, LAST, 5)
-        for r in (5, 6, 7):
+            reopen(r + BANKS)
+        for r in (4, 5):
             finish(r)
-        store(4)
-        quantise(LAST, 5)
-        for r in (10, 11):
-            multiply(LAST, r)
-
-        finish_aside(8)
-        for r in (9, 10, 11):
+        nc.sync.dma_start(out=out_view[:, half(0), :], in_=o_sb[0][:])
+        for u in (4, 5):
+            quantise(2, u)
+        for r in range(BANKS, TILES):
+            multiply(2, r)
+        finish_aside(6)
+        finish_aside(7, left)
+        finish(7, right)
+        for r in (8, 9, 10, 11):
             finish(r)
-        store(8)
+        nc.sync.dma_start(out=out_view[:, half(1), :], in_=o_sb[1][:])

@@ -18,10 +18,10 @@ TILES = T // P
 BANKS = 8
 FLOPS = 2 * K * T * D
 BYTES = 4 * K * T + 2 * 4 * T * D + 1024 * D + 512 * D // 2 + 48 * D
-WIDTH = [4, 4, 2]
-BANK = [0, 1, 2, 3, 4, 5, 6, 7, 0, 1, 2, 3]
-SPLIT = 384
-HALF = TILES // 2
+FIRST, MIDDLE, LAST = 2, 0, 1
+WIDTH = [4, 2, 4]
+PIECE = 3
+SHARE = 32
 
 
 def tile_mix_dyq_tm_mul_kernel(tc, dy, w8_words, w8_scales, w4_words, w4_scales, g, out):
@@ -33,19 +33,18 @@ def tile_mix_dyq_tm_mul_kernel(tc, dy, w8_words, w8_scales, w4_words, w4_scales,
 
         g_view = g.rearrange("(p r) d -> p r d", r=TILES)
         out_view = out.rearrange("(p r) d -> p r d", r=TILES)
+        word_rows = [w8_words[a].rearrange("p n t -> p (n t)") for a in range(2)] + [w4_words[0]]
+        formats = [E4M3X4, E4M3X4, E2M1X4]
 
-        raw8 = keep.tile([P, 2, 4 * T], F32, name="raw8", align_bytes=256)
-        raw4 = keep.tile([P, 4 * T], F32, name="raw4", align_bytes=256)
-        words8 = keep.tile([P, 2, 4 * D], U8, name="words8", align_bytes=256)
-        words4 = keep.tile([P, 2 * D], U8, name="words4", align_bytes=256)
+        raw = [keep.tile([P, 4 * T], F32, name="raw%d" % a, align_bytes=256) for a in range(3)]
+        words = [keep.tile([P, word_rows[a].shape[1]], U8, name="words%d" % a, align_bytes=256) for a in range(3)]
         plane8 = keep.tile([P, 2, D], U8, name="plane8", align_bytes=256)
         plane4 = keep.tile([P, D], U8, name="plane4", align_bytes=256)
-        g_sb = [keep.tile([P, HALF, D], F32, name="g%d" % h, align_bytes=256) for h in range(2)]
-        o_sb = [keep.tile([P, HALF, D], F32, name="o%d" % h, align_bytes=256) for h in range(2)]
-        raw = [raw8[:, 0, :], raw8[:, 1, :], raw4[:, :]]
-        words = [words8[:, 0, :].bitcast(E4M3X4), words8[:, 1, :].bitcast(E4M3X4), words4[:, :].bitcast(E2M1X4)]
+        staged = keep.tile([P, D], U8, name="staged", align_bytes=256)
         planes = [plane8[:, 0, :], plane8[:, 1, :], plane4[:, :]]
-        grouped, codes, scales, acc, sums = {}, {}, {}, {}, {}
+        g_sb = [keep.tile([P, PIECE, D], F32, name="g%d" % n, align_bytes=256) for n in range(TILES // PIECE)]
+        o_sb = [keep.tile([P, PIECE, D], F32, name="o%d" % n, align_bytes=256) for n in range(TILES // PIECE)]
+        grouped, codes, scales, acc = {}, {}, {}, {}
         for a in range(3):
             n = WIDTH[a]
             for u in range(TILES // n):
@@ -53,117 +52,128 @@ def tile_mix_dyq_tm_mul_kernel(tc, dy, w8_words, w8_scales, w4_words, w4_scales,
                 codes[a, u] = keep.tile([P, n * P], U32, name="codes%d_%d" % (a, u), align_bytes=256)
                 scales[a, u] = keep.tile([P, n * P], U8, name="scales%d_%d" % (a, u), align_bytes=256)
 
-        def group(copy, a, u):
+        def group(copy, a, u, m=slice(0, P)):
             n = WIDTH[a]
-            src = raw[a].rearrange("p (j m u i) -> p u m j i", j=4, u=TILES // n, i=n)[:, u]
-            copy(out=grouped[a, u][:].rearrange("p (i m j) -> p m j i", i=n, j=4), in_=src)
+            src = raw[a][:].rearrange("p (j m u i) -> p u m j i", j=4, u=TILES // n, i=n)[:, u]
+            copy(out=grouped[a, u][:].rearrange("p (i m j) -> p m j i", i=n, j=4)[:, m], in_=src[:, m])
 
         def quantise(a, u):
             nc.vector.quantize_mx(out=codes[a, u][:].bitcast(E5M2X4), scales=scales[a, u][:], in_=grouped[a, u][:])
 
         def multiply(a, r):
-            if a == 0:
-                acc[r] = psum.tile([P, D], F32, name="acc%d" % BANK[r])
+            if a == FIRST:
+                acc[r] = psum.tile([P, D], F32, name="acc%d" % (r % BANKS))
             u, i = divmod(r, WIDTH[a])
             cols = slice(P * i, P * (i + 1))
             nc.tensor.matmul_mx(
                 out=acc[r][:],
                 lhsT=codes[a, u][:, cols].bitcast(E5M2X4),
                 lhsT_scale=scales[a, u][:, cols],
-                rhs=words[a],
+                rhs=words[a][:].bitcast(formats[a]),
                 rhs_scale=planes[a],
-                start=(a == 0),
-                stop=(a == 2),
+                start=(a == FIRST),
+                stop=(a == LAST),
             )
 
         def reopen(r):
-            for a in range(2):
-                multiply(a, r)
+            multiply(FIRST, r + BANKS)
+            multiply(MIDDLE, r + BANKS)
 
-        def finish(r, cols=slice(0, D)):
-            h, i = divmod(r, HALF)
-            nc.vector.tensor_tensor(out=o_sb[h][:, i, cols], in0=acc[r][:, cols], in1=g_sb[h][:, i, cols], op=MULT)
+        def finish(r):
+            n, i = divmod(r, PIECE)
+            nc.vector.tensor_tensor(out=o_sb[n][:, i, :], in0=acc[r][:], in1=g_sb[n][:, i, :], op=MULT)
 
-        def set_aside(r, cols=slice(0, D)):
-            sums[r] = keep.tile([P, D], F32, name="sums%d" % r, align_bytes=256)
-            nc.scalar.copy(out=sums[r][:, cols], in_=acc[r][:, cols])
+        def finish_aside(r):
+            n, i = divmod(r, PIECE)
+            sums = keep.tile([P, D], F32, name="sums%d" % r, align_bytes=256)
+            nc.scalar.copy(out=sums[:], in_=acc[r][:])
+            nc.gpsimd.tensor_tensor(out=o_sb[n][:, i, :], in0=sums[:], in1=g_sb[n][:, i, :], op=MULT)
 
-        def finish_aside(r, cols=slice(0, D)):
-            h, i = divmod(r, HALF)
-            nc.gpsimd.tensor_tensor(out=o_sb[h][:, i, cols], in0=sums[r][:, cols], in1=g_sb[h][:, i, cols], op=MULT)
+        def load_dy(a):
+            nc.sync.dma_start(out=raw[a][:], in_=dy[512 * a : 512 * (a + 1), :].rearrange("(p j) t -> p (j t)", j=4))
 
-        left, right = slice(0, SPLIT), slice(SPLIT, D)
+        def load_words(a):
+            nc.sync.dma_start(out=words[a][:].bitcast(I32), in_=word_rows[a].bitcast(I32))
 
-        def half(h):
-            return slice(HALF * h, HALF * (h + 1))
+        def load_w8_scale_rows(r, passes):
+            nc.sync.dma_start(
+                out=plane8[r:P:32, passes, :].bitcast(I32),
+                in_=w8_scales[passes, r:16:4, :].rearrange("a q n -> q a n").bitcast(I32),
+            )
 
+        def load_g(n):
+            nc.sync.dma_start(out=g_sb[n][:], in_=g_view[:, PIECE * n : PIECE * (n + 1), :])
+
+        def store(n):
+            nc.sync.dma_start(out=out_view[:, PIECE * n : PIECE * (n + 1), :], in_=o_sb[n][:])
+
+        for r in range(4):
+            nc.scalar.dma_start(out=staged[r:P:32, :].bitcast(I32), in_=w4_scales[0][r:16:4, :].bitcast(I32))
         nc.vector.memset(plane8[:].bitcast(I32), 0)
         nc.vector.memset(plane4[:].bitcast(I32), 0)
-        nc.sync.dma_start(out=raw8[:], in_=dy[0:1024, :].rearrange("(a p j) t -> p a (j t)", a=2, j=4))
-        nc.sync.dma_start(out=words8[:].bitcast(I32), in_=w8_words.rearrange("a p n t -> p a (n t)").bitcast(I32))
-        for r in range(4):
-            nc.sync.dma_start(
-                out=plane8[r:P:32, :, :].bitcast(I32), in_=w8_scales[:, r:16:4, :].rearrange("a q n -> q a n").bitcast(I32)
-            )
-        nc.sync.dma_start(out=raw4[:], in_=dy[1024:K, :].rearrange("(p j) t -> p (j t)", j=4))
-        nc.sync.dma_start(out=words4[:].bitcast(I32), in_=w4_words[0].bitcast(I32))
-        for r in range(4):
-            nc.sync.dma_start(out=plane4[r:P:32, :].bitcast(I32), in_=w4_scales[0][r:16:4, :].bitcast(I32))
-        for h in range(2):
-            nc.sync.dma_start(out=g_sb[h][:], in_=g_view[:, half(h), :])
+        load_dy(FIRST)
+        load_words(FIRST)
+        load_w8_scale_rows(0, slice(0, 1))
+        load_dy(MIDDLE)
+        load_words(MIDDLE)
+        load_w8_scale_rows(0, slice(1, 2))
+        for r in (1, 2, 3):
+            load_w8_scale_rows(r, slice(0, 2))
+        load_dy(LAST)
+        load_words(LAST)
+        for n in range(TILES // PIECE):
+            load_g(n)
+        for q in range(4):
+            live = slice(32 * q, 32 * q + 4)
+            nc.vector.tensor_copy(out=plane4[live].bitcast(I32), in_=staged[live].bitcast(I32))
 
-        group(nc.scalar.copy, 0, 1)
-        group(nc.scalar.copy, 1, 1)
-        group(nc.scalar.copy, 1, 2)
-        group(nc.vector.tensor_copy, 0, 0)
-        group(nc.vector.tensor_copy, 1, 0)
-        quantise(0, 0)
-        quantise(1, 0)
-        group(nc.vector.tensor_copy, 0, 2)
-        quantise(0, 1)
-        quantise(1, 1)
-        quantise(0, 2)
-        quantise(1, 2)
-        for quad in range(2):
-            for a in range(2):
-                for r in range(4 * quad, 4 * quad + 4):
-                    multiply(a, r)
-
-        group(nc.scalar.copy, 2, 2)
-        group(nc.scalar.copy, 2, 4)
-        group(nc.vector.tensor_copy, 2, 0)
-        group(nc.vector.tensor_copy, 2, 1)
-        quantise(2, 0)
-        quantise(2, 1)
-        group(nc.vector.tensor_copy, 2, 3)
-        for u in (2, 3):
-            quantise(2, u)
+        group(nc.scalar.copy, FIRST, 1)
+        group(nc.scalar.copy, FIRST, 2)
+        group(nc.vector.tensor_copy, FIRST, 0)
+        for u in range(3):
+            quantise(FIRST, u)
         for r in range(BANKS):
-            multiply(2, r)
+            multiply(FIRST, r)
 
-        set_aside(0)
-        set_aside(1, left)
-        group(nc.scalar.copy, 2, 5)
-        reopen(8)
-        set_aside(6)
-        set_aside(7, left)
+        group(nc.vector.tensor_copy, MIDDLE, 2, slice(0, SHARE))
+        group(nc.scalar.copy, MIDDLE, 2, slice(SHARE, P))
+        quantise(MIDDLE, 2)
+        for u in (0, 1):
+            group(nc.scalar.copy, MIDDLE, u)
+            quantise(MIDDLE, u)
+        for r in range(BANKS):
+            multiply(MIDDLE, r)
+
+        for u in (2, 3):
+            group(nc.scalar.copy, LAST, u)
+        for u in (0, 1):
+            group(nc.vector.tensor_copy, LAST, u)
+        for u in range(4):
+            quantise(LAST, u)
+        for r in range(BANKS):
+            multiply(LAST, r)
+
         finish_aside(0)
-        finish_aside(1, left)
-        finish(1, right)
-        reopen(9)
-        for r in (2, 3):
+        reopen(0)
+        group(nc.scalar.copy, LAST, 4)
+        for r in (1, 2):
             finish(r)
-            reopen(r + BANKS)
+            reopen(r)
+        store(0)
+        quantise(LAST, 4)
+        finish_aside(3)
+        for r in (8, 9):
+            multiply(LAST, r)
+        reopen(3)
+        group(nc.scalar.copy, LAST, 5)
         for r in (4, 5):
             finish(r)
-        nc.sync.dma_start(out=out_view[:, half(0), :], in_=o_sb[0][:])
-        for u in (4, 5):
-            quantise(2, u)
-        for r in range(BANKS, TILES):
-            multiply(2, r)
-        finish_aside(6)
-        finish_aside(7, left)
-        finish(7, right)
-        for r in (8, 9, 10, 11):
-            finish(r)
-        nc.sync.dma_start(out=out_view[:, half(1), :], in_=o_sb[1][:])
+        store(1)
+        quantise(LAST, 5)
+        for r in (10, 11):
+            multiply(LAST, r)
+        for n in (2, 3):
+            finish_aside(PIECE * n)
+            for r in (PIECE * n + 1, PIECE * n + 2):
+                finish(r)
+            store(n)

@@ -18,10 +18,10 @@ TILES = T // P
 BANKS = 8
 FLOPS = 2 * K * T * D
 BYTES = 4 * K * T + 2 * 4 * T * D + 1024 * D + 512 * D // 2 + 48 * D
-FIRST, MIDDLE, LAST = 2, 0, 1
-WIDTH = [4, 2, 4]
-PIECE = 3
-SHARE = 32
+FIRST, MIDDLE, LAST = 0, 1, 2
+WIDTH = [4, 4, 2]
+PIECE = 4
+SHARE = 48
 
 
 def tile_mix_dyq_tm_mul_kernel(tc, dy, w8_words, w8_scales, w4_words, w4_scales, g, out):
@@ -33,15 +33,14 @@ def tile_mix_dyq_tm_mul_kernel(tc, dy, w8_words, w8_scales, w4_words, w4_scales,
 
         g_view = g.rearrange("(p r) d -> p r d", r=TILES)
         out_view = out.rearrange("(p r) d -> p r d", r=TILES)
-        word_rows = [w8_words[a].rearrange("p n t -> p (n t)") for a in range(2)] + [w4_words[0]]
-        formats = [E4M3X4, E4M3X4, E2M1X4]
 
         raw = [keep.tile([P, 4 * T], F32, name="raw%d" % a, align_bytes=256) for a in range(3)]
-        words = [keep.tile([P, word_rows[a].shape[1]], U8, name="words%d" % a, align_bytes=256) for a in range(3)]
-        plane8 = keep.tile([P, 2, D], U8, name="plane8", align_bytes=256)
-        plane4 = keep.tile([P, D], U8, name="plane4", align_bytes=256)
+        words8 = keep.tile([P, 2, 4 * D], U8, name="words8", align_bytes=256)
+        words4 = keep.tile([P, 2 * D], U8, name="words4", align_bytes=256)
+        words = [words8[:, 0, :].bitcast(E4M3X4), words8[:, 1, :].bitcast(E4M3X4), words4[:, :].bitcast(E2M1X4)]
+        scale_rows = [w8_scales[0], w8_scales[1], w4_scales[0]]
+        planes = [keep.tile([P, D], U8, name="plane%d" % a, align_bytes=256) for a in range(3)]
         staged = keep.tile([P, D], U8, name="staged", align_bytes=256)
-        planes = [plane8[:, 0, :], plane8[:, 1, :], plane4[:, :]]
         g_sb = [keep.tile([P, PIECE, D], F32, name="g%d" % n, align_bytes=256) for n in range(TILES // PIECE)]
         o_sb = [keep.tile([P, PIECE, D], F32, name="o%d" % n, align_bytes=256) for n in range(TILES // PIECE)]
         grouped, codes, scales, acc = {}, {}, {}, {}
@@ -69,8 +68,8 @@ def tile_mix_dyq_tm_mul_kernel(tc, dy, w8_words, w8_scales, w4_words, w4_scales,
                 out=acc[r][:],
                 lhsT=codes[a, u][:, cols].bitcast(E5M2X4),
                 lhsT_scale=scales[a, u][:, cols],
-                rhs=words[a][:].bitcast(formats[a]),
-                rhs_scale=planes[a],
+                rhs=words[a],
+                rhs_scale=planes[a][:],
                 start=(a == FIRST),
                 stop=(a == LAST),
             )
@@ -92,14 +91,9 @@ def tile_mix_dyq_tm_mul_kernel(tc, dy, w8_words, w8_scales, w4_words, w4_scales,
         def load_dy(a):
             nc.sync.dma_start(out=raw[a][:], in_=dy[512 * a : 512 * (a + 1), :].rearrange("(p j) t -> p (j t)", j=4))
 
-        def load_words(a):
-            nc.sync.dma_start(out=words[a][:].bitcast(I32), in_=word_rows[a].bitcast(I32))
-
-        def load_w8_scale_rows(r, passes):
-            nc.sync.dma_start(
-                out=plane8[r:P:32, passes, :].bitcast(I32),
-                in_=w8_scales[passes, r:16:4, :].rearrange("a q n -> q a n").bitcast(I32),
-            )
+        def load_scale_rows(queue, dst, a, which):
+            for r in which:
+                queue.dma_start(out=dst[r:P:32, :].bitcast(I32), in_=scale_rows[a][r:16:4, :].bitcast(I32))
 
         def load_g(n):
             nc.sync.dma_start(out=g_sb[n][:], in_=g_view[:, PIECE * n : PIECE * (n + 1), :])
@@ -107,25 +101,22 @@ def tile_mix_dyq_tm_mul_kernel(tc, dy, w8_words, w8_scales, w4_words, w4_scales,
         def store(n):
             nc.sync.dma_start(out=out_view[:, PIECE * n : PIECE * (n + 1), :], in_=o_sb[n][:])
 
-        for r in range(4):
-            nc.scalar.dma_start(out=staged[r:P:32, :].bitcast(I32), in_=w4_scales[0][r:16:4, :].bitcast(I32))
-        nc.vector.memset(plane8[:].bitcast(I32), 0)
-        nc.vector.memset(plane4[:].bitcast(I32), 0)
+        load_scale_rows(nc.scalar, staged, FIRST, range(4))
+        for a in (MIDDLE, LAST, FIRST):
+            nc.vector.memset(planes[a][:].bitcast(I32), 0)
         load_dy(FIRST)
-        load_words(FIRST)
-        load_w8_scale_rows(0, slice(0, 1))
+        nc.sync.dma_start(out=words8[:].bitcast(I32), in_=w8_words.rearrange("a p n t -> p a (n t)").bitcast(I32))
+        load_scale_rows(nc.sync, planes[MIDDLE], MIDDLE, range(1))
         load_dy(MIDDLE)
-        load_words(MIDDLE)
-        load_w8_scale_rows(0, slice(1, 2))
-        for r in (1, 2, 3):
-            load_w8_scale_rows(r, slice(0, 2))
+        load_scale_rows(nc.sync, planes[MIDDLE], MIDDLE, range(1, 4))
         load_dy(LAST)
-        load_words(LAST)
+        nc.sync.dma_start(out=words4[:].bitcast(I32), in_=w4_words[0].bitcast(I32))
+        load_scale_rows(nc.sync, planes[LAST], LAST, range(4))
         for n in range(TILES // PIECE):
             load_g(n)
         for q in range(4):
             live = slice(32 * q, 32 * q + 4)
-            nc.vector.tensor_copy(out=plane4[live].bitcast(I32), in_=staged[live].bitcast(I32))
+            nc.vector.tensor_copy(out=planes[FIRST][live].bitcast(I32), in_=staged[live].bitcast(I32))
 
         group(nc.scalar.copy, FIRST, 1)
         group(nc.scalar.copy, FIRST, 2)
@@ -156,24 +147,24 @@ def tile_mix_dyq_tm_mul_kernel(tc, dy, w8_words, w8_scales, w4_words, w4_scales,
         finish_aside(0)
         reopen(0)
         group(nc.scalar.copy, LAST, 4)
-        for r in (1, 2):
+        for r in (1, 2, 3):
             finish(r)
             reopen(r)
         store(0)
         quantise(LAST, 4)
-        finish_aside(3)
         for r in (8, 9):
             multiply(LAST, r)
-        reopen(3)
+
+        finish_aside(4)
         group(nc.scalar.copy, LAST, 5)
-        for r in (4, 5):
+        for r in (5, 6, 7):
             finish(r)
         store(1)
         quantise(LAST, 5)
         for r in (10, 11):
             multiply(LAST, r)
-        for n in (2, 3):
-            finish_aside(PIECE * n)
-            for r in (PIECE * n + 1, PIECE * n + 2):
-                finish(r)
-            store(n)
+
+        finish_aside(8)
+        for r in (9, 10, 11):
+            finish(r)
+        store(2)

@@ -19,9 +19,10 @@ BANKS = 8
 FLOPS = 2 * K * T * D
 BYTES = 4 * K * T + 2 * 4 * T * D + 1024 * D + 512 * D // 2 + 48 * D
 FIRST, MIDDLE, LAST = 0, 1, 2
-WIDTH = [4, 4, 2]
+QUAD = 4
 PIECE = 4
-SHARE = 48
+LAST_SHARE = [80, 64]
+SHARE = 96
 
 
 def tile_mix_dyq_tm_mul_kernel(tc, dy, w8_words, w8_scales, w4_words, w4_scales, g, out):
@@ -45,24 +46,28 @@ def tile_mix_dyq_tm_mul_kernel(tc, dy, w8_words, w8_scales, w4_words, w4_scales,
         o_sb = [keep.tile([P, PIECE, D], F32, name="o%d" % n, align_bytes=256) for n in range(TILES // PIECE)]
         grouped, codes, scales, acc = {}, {}, {}, {}
         for a in range(3):
-            n = WIDTH[a]
-            for u in range(TILES // n):
-                grouped[a, u] = keep.tile([P, n * D], BF16, name="grouped%d_%d" % (a, u), align_bytes=256)
-                codes[a, u] = keep.tile([P, n * P], U32, name="codes%d_%d" % (a, u), align_bytes=256)
-                scales[a, u] = keep.tile([P, n * P], U8, name="scales%d_%d" % (a, u), align_bytes=256)
+            for u in range(TILES // QUAD):
+                grouped[a, u] = keep.tile([P, QUAD * D], BF16, name="grouped%d_%d" % (a, u), align_bytes=256)
+                codes[a, u] = keep.tile([P, QUAD * P], U32, name="codes%d_%d" % (a, u), align_bytes=256)
+                scales[a, u] = keep.tile([P, QUAD * P], U8, name="scales%d_%d" % (a, u), align_bytes=256)
 
-        def group(copy, a, u, m=slice(0, P)):
-            n = WIDTH[a]
-            src = raw[a][:].rearrange("p (j m u i) -> p u m j i", j=4, u=TILES // n, i=n)[:, u]
-            copy(out=grouped[a, u][:].rearrange("p (i m j) -> p m j i", i=n, j=4)[:, m], in_=src[:, m])
+        def group(copy, a, u, m=slice(0, P), i=slice(0, QUAD)):
+            src = raw[a][:].rearrange("p (j m u i) -> p u m j i", j=4, u=TILES // QUAD, i=QUAD)[:, u]
+            dst = grouped[a, u][:].rearrange("p (i m j) -> p m j i", i=QUAD, j=4)
+            copy(out=dst[:, m, :, i], in_=src[:, m, :, i])
 
-        def quantise(a, u):
-            nc.vector.quantize_mx(out=codes[a, u][:].bitcast(E5M2X4), scales=scales[a, u][:], in_=grouped[a, u][:])
+        def quantise(a, u, i=slice(0, QUAD)):
+            cols = slice(P * i.start, P * i.stop)
+            nc.vector.quantize_mx(
+                out=codes[a, u][:, cols].bitcast(E5M2X4),
+                scales=scales[a, u][:, cols],
+                in_=grouped[a, u][:, D * i.start : D * i.stop],
+            )
 
         def multiply(a, r):
             if a == FIRST:
                 acc[r] = psum.tile([P, D], F32, name="acc%d" % (r % BANKS))
-            u, i = divmod(r, WIDTH[a])
+            u, i = divmod(r, QUAD)
             cols = slice(P * i, P * (i + 1))
             nc.tensor.matmul_mx(
                 out=acc[r][:],
@@ -135,32 +140,33 @@ def tile_mix_dyq_tm_mul_kernel(tc, dy, w8_words, w8_scales, w4_words, w4_scales,
         for r in range(BANKS):
             multiply(MIDDLE, r)
 
-        for u in (2, 3):
-            group(nc.scalar.copy, LAST, u)
+        front, back = slice(0, QUAD // 2), slice(QUAD // 2, QUAD)
         for u in (0, 1):
-            group(nc.vector.tensor_copy, LAST, u)
-        for u in range(4):
-            quantise(LAST, u)
+            group(nc.vector.tensor_copy, LAST, u, slice(0, LAST_SHARE[u]))
+            group(nc.scalar.copy, LAST, u, slice(LAST_SHARE[u], P))
+        for u in (0, 1):
+            quantise(LAST, u, front)
+            quantise(LAST, u, back)
         for r in range(BANKS):
             multiply(LAST, r)
 
         finish_aside(0)
         reopen(0)
-        group(nc.scalar.copy, LAST, 4)
+        group(nc.scalar.copy, LAST, 2, i=front)
         for r in (1, 2, 3):
             finish(r)
             reopen(r)
         store(0)
-        quantise(LAST, 4)
+        quantise(LAST, 2, front)
         for r in (8, 9):
             multiply(LAST, r)
 
         finish_aside(4)
-        group(nc.scalar.copy, LAST, 5)
+        group(nc.scalar.copy, LAST, 2, i=back)
         for r in (5, 6, 7):
             finish(r)
         store(1)
-        quantise(LAST, 5)
+        quantise(LAST, 2, back)
         for r in (10, 11):
             multiply(LAST, r)
 

@@ -43,25 +43,36 @@ def tile_mix_dyq_tm_mul_kernel(tc, dy, w8_words, w8_scales, w4_words, w4_scales,
         planes = [keep.tile([P, D], U8, name="plane%d" % a, align_bytes=256) for a in range(3)]
         staged = keep.tile([P, D], U8, name="staged", align_bytes=256)
         g_sb = [keep.tile([P, PIECE, D], F32, name="g%d" % n, align_bytes=256) for n in range(TILES // PIECE)]
-        o_sb = [keep.tile([P, PIECE, D], F32, name="o%d" % n, align_bytes=256) for n in range(TILES // PIECE)]
+        front, back = slice(0, QUAD // 2), slice(QUAD // 2, QUAD)
+        o_first = keep.tile([P, (PIECE + 1) * D], F32, name="o0", align_bytes=256)
+        o_sb = [o_first[:, D:]] + [keep.tile([P, PIECE * D], F32, name="o%d" % n, align_bytes=256)[:, :] for n in (1, 2)]
         grouped, codes, scales, acc = {}, {}, {}, {}
         for a in range(3):
             for u in range(TILES // QUAD):
-                grouped[a, u] = keep.tile([P, QUAD * D], BF16, name="grouped%d_%d" % (a, u), align_bytes=256)
+                if a != LAST or u == 0:
+                    grouped[a, u] = keep.tile([P, QUAD * D], BF16, name="grouped%d_%d" % (a, u), align_bytes=256)[:, :]
                 codes[a, u] = keep.tile([P, QUAD * P], U32, name="codes%d_%d" % (a, u), align_bytes=256)
                 scales[a, u] = keep.tile([P, QUAD * P], U8, name="scales%d_%d" % (a, u), align_bytes=256)
 
-        def group(copy, a, u, m=slice(0, P), i=slice(0, QUAD)):
-            src = raw[a][:].rearrange("p (j m u i) -> p u m j i", j=4, u=TILES // QUAD, i=QUAD)[:, u]
-            dst = grouped[a, u][:].rearrange("p (i m j) -> p m j i", i=QUAD, j=4)
-            copy(out=dst[:, m, :, i], in_=src[:, m, :, i])
+        grouped[LAST, 1] = o_first[:, : 2 * D].bitcast(BF16)
+        pairs = [o_sb[n][:, :D].bitcast(BF16) for n in (1, 2)]
 
-        def quantise(a, u, i=slice(0, QUAD)):
+        def quad_rows(a, u):
+            return raw[a][:].rearrange("p (j m u i) -> p u m j i", j=4, u=TILES // QUAD, i=QUAD)[:, u]
+
+        def group(copy, a, u, m=slice(0, P)):
+            dst = grouped[a, u].rearrange("p (i m j) -> p m j i", i=QUAD, j=4)
+            copy(out=dst[:, m], in_=quad_rows(a, u)[:, m])
+
+        def group_pair(h, i):
+            nc.scalar.copy(out=pairs[h].rearrange("p (i m j) -> p m j i", i=2, j=4), in_=quad_rows(LAST, 2)[:, :, :, i])
+
+        def quantise(a, u, i=slice(0, QUAD), values=None):
             cols = slice(P * i.start, P * i.stop)
             nc.vector.quantize_mx(
                 out=codes[a, u][:, cols].bitcast(E5M2X4),
                 scales=scales[a, u][:, cols],
-                in_=grouped[a, u][:, D * i.start : D * i.stop],
+                in_=grouped[a, u][:, D * i.start : D * i.stop] if values is None else values,
             )
 
         def multiply(a, r):
@@ -85,13 +96,13 @@ def tile_mix_dyq_tm_mul_kernel(tc, dy, w8_words, w8_scales, w4_words, w4_scales,
 
         def finish(r):
             n, i = divmod(r, PIECE)
-            nc.vector.tensor_tensor(out=o_sb[n][:, i, :], in0=acc[r][:], in1=g_sb[n][:, i, :], op=MULT)
+            nc.vector.tensor_tensor(out=o_sb[n][:, D * i : D * (i + 1)], in0=acc[r][:], in1=g_sb[n][:, i, :], op=MULT)
 
         def finish_aside(r):
             n, i = divmod(r, PIECE)
             sums = keep.tile([P, D], F32, name="sums%d" % r, align_bytes=256)
             nc.scalar.copy(out=sums[:], in_=acc[r][:])
-            nc.gpsimd.tensor_tensor(out=o_sb[n][:, i, :], in0=sums[:], in1=g_sb[n][:, i, :], op=MULT)
+            nc.gpsimd.tensor_tensor(out=o_sb[n][:, D * i : D * (i + 1)], in0=sums[:], in1=g_sb[n][:, i, :], op=MULT)
 
         def load_dy(a):
             nc.sync.dma_start(out=raw[a][:], in_=dy[512 * a : 512 * (a + 1), :].rearrange("(p j) t -> p (j t)", j=4))
@@ -104,7 +115,7 @@ def tile_mix_dyq_tm_mul_kernel(tc, dy, w8_words, w8_scales, w4_words, w4_scales,
             nc.sync.dma_start(out=g_sb[n][:], in_=g_view[:, PIECE * n : PIECE * (n + 1), :])
 
         def store(n):
-            nc.sync.dma_start(out=out_view[:, PIECE * n : PIECE * (n + 1), :], in_=o_sb[n][:])
+            nc.sync.dma_start(out=out_view[:, PIECE * n : PIECE * (n + 1), :], in_=o_sb[n].rearrange("p (r d) -> p r d", d=D))
 
         load_scale_rows(nc.scalar, staged, FIRST, range(4))
         for a in (MIDDLE, LAST, FIRST):
@@ -140,7 +151,6 @@ def tile_mix_dyq_tm_mul_kernel(tc, dy, w8_words, w8_scales, w4_words, w4_scales,
         for r in range(BANKS):
             multiply(MIDDLE, r)
 
-        front, back = slice(0, QUAD // 2), slice(QUAD // 2, QUAD)
         for u in (0, 1):
             group(nc.vector.tensor_copy, LAST, u, slice(0, LAST_SHARE[u]))
             group(nc.scalar.copy, LAST, u, slice(LAST_SHARE[u], P))
@@ -152,21 +162,21 @@ def tile_mix_dyq_tm_mul_kernel(tc, dy, w8_words, w8_scales, w4_words, w4_scales,
 
         finish_aside(0)
         reopen(0)
-        group(nc.scalar.copy, LAST, 2, i=front)
+        group_pair(0, front)
         for r in (1, 2, 3):
             finish(r)
             reopen(r)
         store(0)
-        quantise(LAST, 2, front)
+        quantise(LAST, 2, front, pairs[0])
         for r in (8, 9):
             multiply(LAST, r)
 
         finish_aside(4)
-        group(nc.scalar.copy, LAST, 2, i=back)
+        group_pair(1, back)
         for r in (5, 6, 7):
             finish(r)
         store(1)
-        quantise(LAST, 2, back)
+        quantise(LAST, 2, back, pairs[1])
         for r in (10, 11):
             multiply(LAST, r)
 

from contextlib import ExitStack

import concourse.mybir as mybir

F32 = mybir.dt.float32
BF16 = mybir.dt.bfloat16
U32 = mybir.dt.uint32
I32 = mybir.dt.int32
U8 = mybir.dt.uint8
E4M3X4 = mybir.dt.float8_e4m3fn_x4
E5M2X4 = mybir.dt.float8_e5m2_x4
E2M1X4 = mybir.dt.float4_e2m1fn_x4
MULT = mybir.AluOpType.mult

P = 128
K, T, D = 1536, 1536, 512
TILES = T // P
BANKS = 8
FLOPS = 2 * K * T * D
BYTES = 4 * K * T + 2 * 4 * T * D + 1024 * D + 512 * D // 2 + 48 * D
FIRST, MIDDLE, LAST = 0, 1, 2
QUAD = 4
PIECE = 4
LAST_SHARE = [80, 64]
SHARE = 96


def tile_mix_dyq_tm_mul_kernel(tc, dy, w8_words, w8_scales, w4_words, w4_scales, g, out):
    nc = tc.nc
    with ExitStack() as ctx:
        keep = ctx.enter_context(tc.tile_pool(name="keep", bufs=1))
        psum = ctx.enter_context(tc.psum_pool(name="psum", bufs=1))
        ctx.enter_context(tc.manual_schedule())

        g_view = g.rearrange("(p r) d -> p r d", r=TILES)
        out_view = out.rearrange("(p r) d -> p r d", r=TILES)

        raw = [keep.tile([P, 4 * T], F32, name="raw%d" % a, align_bytes=256) for a in range(3)]
        words8 = keep.tile([P, 2, 4 * D], U8, name="words8", align_bytes=256)
        words4 = keep.tile([P, 2 * D], U8, name="words4", align_bytes=256)
        words = [words8[:, 0, :].bitcast(E4M3X4), words8[:, 1, :].bitcast(E4M3X4), words4[:, :].bitcast(E2M1X4)]
        scale_rows = [w8_scales[0], w8_scales[1], w4_scales[0]]
        planes = [keep.tile([P, D], U8, name="plane%d" % a, align_bytes=256) for a in range(3)]
        staged = keep.tile([P, D], U8, name="staged", align_bytes=256)
        g_sb = [keep.tile([P, PIECE, D], F32, name="g%d" % n, align_bytes=256) for n in range(TILES // PIECE)]
        front, back = slice(0, QUAD // 2), slice(QUAD // 2, QUAD)
        o_first = keep.tile([P, (PIECE + 1) * D], F32, name="o0", align_bytes=256)
        o_sb = [o_first[:, D:]] + [keep.tile([P, PIECE * D], F32, name="o%d" % n, align_bytes=256)[:, :] for n in (1, 2)]
        grouped, codes, scales, acc = {}, {}, {}, {}
        for a in range(3):
            for u in range(TILES // QUAD):
                if a != LAST or u == 0:
                    grouped[a, u] = keep.tile([P, QUAD * D], BF16, name="grouped%d_%d" % (a, u), align_bytes=256)[:, :]
                codes[a, u] = keep.tile([P, QUAD * P], U32, name="codes%d_%d" % (a, u), align_bytes=256)
                scales[a, u] = keep.tile([P, QUAD * P], U8, name="scales%d_%d" % (a, u), align_bytes=256)

        grouped[LAST, 1] = o_first[:, : 2 * D].bitcast(BF16)
        pairs = [o_sb[n][:, :D].bitcast(BF16) for n in (1, 2)]

        def quad_rows(a, u):
            return raw[a][:].rearrange("p (j m u i) -> p u m j i", j=4, u=TILES // QUAD, i=QUAD)[:, u]

        def group(copy, a, u, m=slice(0, P)):
            dst = grouped[a, u].rearrange("p (i m j) -> p m j i", i=QUAD, j=4)
            copy(out=dst[:, m], in_=quad_rows(a, u)[:, m])

        def group_pair(h, i):
            nc.scalar.copy(out=pairs[h].rearrange("p (i m j) -> p m j i", i=2, j=4), in_=quad_rows(LAST, 2)[:, :, :, i])

        def quantise(a, u, i=slice(0, QUAD), values=None):
            cols = slice(P * i.start, P * i.stop)
            nc.vector.quantize_mx(
                out=codes[a, u][:, cols].bitcast(E5M2X4),
                scales=scales[a, u][:, cols],
                in_=grouped[a, u][:, D * i.start : D * i.stop] if values is None else values,
            )

        def multiply(a, r):
            if a == FIRST:
                acc[r] = psum.tile([P, D], F32, name="acc%d" % (r % BANKS))
            u, i = divmod(r, QUAD)
            cols = slice(P * i, P * (i + 1))
            nc.tensor.matmul_mx(
                out=acc[r][:],
                lhsT=codes[a, u][:, cols].bitcast(E5M2X4),
                lhsT_scale=scales[a, u][:, cols],
                rhs=words[a],
                rhs_scale=planes[a][:],
                start=(a == FIRST),
                stop=(a == LAST),
            )

        def reopen(r):
            multiply(FIRST, r + BANKS)
            multiply(MIDDLE, r + BANKS)

        def finish(r):
            n, i = divmod(r, PIECE)
            nc.vector.tensor_tensor(out=o_sb[n][:, D * i : D * (i + 1)], in0=acc[r][:], in1=g_sb[n][:, i, :], op=MULT)

        def finish_aside(r):
            n, i = divmod(r, PIECE)
            sums = keep.tile([P, D], F32, name="sums%d" % r, align_bytes=256)
            nc.scalar.copy(out=sums[:], in_=acc[r][:])
            nc.gpsimd.tensor_tensor(out=o_sb[n][:, D * i : D * (i + 1)], in0=sums[:], in1=g_sb[n][:, i, :], op=MULT)

        def load_dy(a):
            nc.sync.dma_start(out=raw[a][:], in_=dy[512 * a : 512 * (a + 1), :].rearrange("(p j) t -> p (j t)", j=4))

        def load_scale_rows(queue, dst, a, which):
            for r in which:
                queue.dma_start(out=dst[r:P:32, :].bitcast(I32), in_=scale_rows[a][r:16:4, :].bitcast(I32))

        def load_g(n):
            nc.sync.dma_start(out=g_sb[n][:], in_=g_view[:, PIECE * n : PIECE * (n + 1), :])

        def store(n):
            nc.sync.dma_start(out=out_view[:, PIECE * n : PIECE * (n + 1), :], in_=o_sb[n].rearrange("p (r d) -> p r d", d=D))

        load_scale_rows(nc.scalar, staged, FIRST, range(4))
        for a in (MIDDLE, LAST, FIRST):
            nc.vector.memset(planes[a][:].bitcast(I32), 0)
        load_dy(FIRST)
        nc.sync.dma_start(out=words8[:].bitcast(I32), in_=w8_words.rearrange("a p n t -> p a (n t)").bitcast(I32))
        load_scale_rows(nc.sync, planes[MIDDLE], MIDDLE, range(1))
        load_dy(MIDDLE)
        load_scale_rows(nc.sync, planes[MIDDLE], MIDDLE, range(1, 4))
        load_dy(LAST)
        nc.sync.dma_start(out=words4[:].bitcast(I32), in_=w4_words[0].bitcast(I32))
        load_scale_rows(nc.sync, planes[LAST], LAST, range(4))
        for n in range(TILES // PIECE):
            load_g(n)
        for q in range(4):
            live = slice(32 * q, 32 * q + 4)
            nc.vector.tensor_copy(out=planes[FIRST][live].bitcast(I32), in_=staged[live].bitcast(I32))

        group(nc.scalar.copy, FIRST, 1)
        group(nc.scalar.copy, FIRST, 2)
        group(nc.vector.tensor_copy, FIRST, 0)
        for u in range(3):
            quantise(FIRST, u)
        for r in range(BANKS):
            multiply(FIRST, r)

        group(nc.vector.tensor_copy, MIDDLE, 2, slice(0, SHARE))
        group(nc.scalar.copy, MIDDLE, 2, slice(SHARE, P))
        quantise(MIDDLE, 2)
        for u in (0, 1):
            group(nc.scalar.copy, MIDDLE, u)
            quantise(MIDDLE, u)
        for r in range(BANKS):
            multiply(MIDDLE, r)

        for u in (0, 1):
            group(nc.vector.tensor_copy, LAST, u, slice(0, LAST_SHARE[u]))
            group(nc.scalar.copy, LAST, u, slice(LAST_SHARE[u], P))
        for u in (0, 1):
            quantise(LAST, u, front)
            quantise(LAST, u, back)
        for r in range(BANKS):
            multiply(LAST, r)

        finish_aside(0)
        reopen(0)
        group_pair(0, front)
        for r in (1, 2, 3):
            finish(r)
            reopen(r)
        store(0)
        quantise(LAST, 2, front, pairs[0])
        for r in (8, 9):
            multiply(LAST, r)

        finish_aside(4)
        group_pair(1, back)
        for r in (5, 6, 7):
            finish(r)
        store(1)
        quantise(LAST, 2, back, pairs[1])
        for r in (10, 11):
            multiply(LAST, r)

        finish_aside(8)
        for r in (9, 10, 11):
            finish(r)
        store(2)
